import numpy as np
import ml_dtypes


def mxq(x, axis, fmt="e4m3"):
    dtype, down = {"e4m3": (ml_dtypes.float8_e4m3fn, 7), "e5m2": (ml_dtypes.float8_e5m2, 14)}[fmt]
    v = np.moveaxis(np.asarray(x, np.float32).astype(ml_dtypes.bfloat16).astype(np.float64), axis, -1)
    blocks = v.reshape(v.shape[:-1] + (-1, 32))
    amax = np.abs(blocks).max(-1, keepdims=True)
    byte = np.maximum(np.where(amax > 0, np.frexp(amax)[1] - 1 + 127, 0) - down, 1)
    scale = np.exp2(byte - 127.0)
    codes = (blocks / scale).astype(np.float32).astype(dtype).astype(np.float64)
    return np.moveaxis((codes * scale).reshape(v.shape), -1, axis)


WIDE = False


def mx_kscale(k):
    if not WIDE:
        return np.ones(k)
    levels = np.array([10, -10, 5, -5, 0])
    if k % 512:
        return np.exp2(np.random.permutation(np.resize(levels, k // 32))).repeat(32)
    a = np.empty((k // 512, 16))
    for p in range(k // 512):
        a[p, :8] = np.random.permutation(np.resize(levels, 8))
        for g in range(8):
            far = levels[np.abs(levels - a[p, g]) >= 10]
            a[p, g + 8] = far[np.random.randint(len(far))]
    return np.exp2(a.ravel()).repeat(32)


def f64(x):
    return np.asarray(x).astype(np.float64)


def striped(idx):
    return np.tile(idx.reshape(-1, 16).T, (8, 1)).astype(np.uint16)


def unstriped(offs):
    return offs[:16].T.reshape(-1).astype(np.int64)


K, T, S, D, V, N = 1024, 1024, 512, 4, 256, 128
P = 2 ** 7


def setup_inputs():
    n = np.random.standard_normal
    s = mx_kscale(K)[:, None]
    return {
        "xT": (n((K, T)) * s).astype(np.float32),
        "w1": (n((K, N)) / np.sqrt(K) / s).astype(np.float32),
        "gate": (np.tile(np.random.uniform(0.2, 1.0, (D, 1, V)) / np.sqrt(D), (1, P, 1))).astype(np.float32),
        "offs": striped(np.random.permutation(T)[:S]),
        "cen": striped(np.random.permutation(S)[:V]),
        "pos1": striped(np.random.permutation(S)[:V]),
        "pos2": striped(np.random.permutation(S)[:V]),
        "pos3": striped(np.random.permutation(S)[:V]),
        "pos4": striped(np.random.permutation(S)[:V]),
    }


def reference(xT, w1, gate, offs, cen, pos1, pos2, pos3, pos4):
    xq = mxq(f64(xT)[:, unstriped(offs)], 0, "e4m3")
    y = mxq(f64(w1), 0, "e4m3").T @ xq
    yc = y[:, unstriped(cen)]
    return yc + (y[:, unstriped(pos1)] - yc) * f64(gate)[0, :1] + (y[:, unstriped(pos2)] - yc) * f64(gate)[1, :1] + (y[:, unstriped(pos3)] - yc) * f64(gate)[2, :1] + (y[:, unstriped(pos4)] - yc) * f64(gate)[3, :1]

@@ -1,0 +1,195 @@
+from contextlib import ExitStack
+
+import concourse.mybir as mybir
+from concourse.masks import make_identity
+
+K, T, S, D, V, N = 1024, 1024, 512, 4, 256, 128
+P = 128
+PACK = 4
+K_PASS = P * PACK
+PASSES = K // K_PASS
+HALVES = V // P
+STRIPE = 16
+
+FLOPS = 2 * K * N * S
+
+F32 = mybir.dt.float32
+BF16 = mybir.dt.bfloat16
+U32 = mybir.dt.uint32
+I32 = mybir.dt.int32
+U16 = mybir.dt.uint16
+U8 = mybir.dt.uint8
+FP8X4 = mybir.dt.float8_e4m3fn_x4
+COPY = mybir.ActivationFunctionType.Copy
+ADD = mybir.AluOpType.add
+MULT = mybir.AluOpType.mult
+
+CHUNK = 512
+VECTOR_CAST = (320, 320, 320, 256)
+LAST_SLICES = ((0, 256), (256, 384), (384, 512))
+
+
+def tile_picked_grand_none_e_kernel(tc, xT, w1, gate, offs, cen, pos1, pos2, pos3, pos4, out):
+    nc = tc.nc
+    with ExitStack() as ctx:
+        lists = ctx.enter_context(tc.tile_pool(name="lists", bufs=1))
+        keep = ctx.enter_context(tc.tile_pool(name="keep", bufs=1))
+        reuse = ctx.enter_context(tc.tile_pool(name="reuse", bufs=1))
+        psum = ctx.enter_context(tc.psum_pool(name="psum", bufs=1))
+        turn = ctx.enter_context(tc.psum_pool(name="turn", bufs=3))
+
+        x_rows = xT.rearrange("(g p j) t -> g p j t", g=PASSES, j=PACK)
+        x_raw = {}
+        offs_sb = lists.tile([P, S // STRIPE], U16)
+        for g in range(PASSES):
+            for u in range(2):
+                for c in range(T // CHUNK):
+                    if (g, c) == (1, 1):
+                        raw = reuse.tile([P, 2, CHUNK], F32, name="x_raw_reused_%d" % u, align_bytes=64, offset=4096 * u)
+                    else:
+                        raw = keep.tile([P, 2, CHUNK], F32, name="x_raw_%d_%d_%d" % (g, u, c))
+                    nc.sync.dma_start(out=raw[:], in_=x_rows[g, :, 2 * u : 2 * u + 2, c * CHUNK : (c + 1) * CHUNK])
+                    x_raw[g, u, c] = raw
+                    if (g, u, c) == (0, 0, 0):
+                        nc.sync.dma_start(offs_sb[:], offs)
+
+        w_rows = w1.rearrange("(g p j) m -> g p j m", g=PASSES, j=PACK)
+        w_raw = []
+        for g in range(PASSES):
+            raw = keep.tile([P, PACK, N], F32, name="w_raw_%d" % g)
+            nc.sync.dma_start(out=raw[:], in_=w_rows[g])
+            w_raw.append(raw)
+        edge = keep.tile([P, D, HALVES], F32)
+        with nc.allow_non_contiguous_dma(reason="one diffusivity a partition"):
+            gate_halves = gate.rearrange("d r (h v) -> (d r h) v", v=P)
+            nc.sync.dma_start(out=edge[:].rearrange("p d h -> p (d h)"), in_=gate_halves[0 : D * P * HALVES : P + 1, :].rearrange("i p -> p i"))
+        term_lists = []
+        for name, src in (("pos1", pos1), ("pos2", pos2), ("cen", cen), ("pos3", pos3), ("pos4", pos4)):
+            list_sb = lists.tile([P, V // STRIPE], U16, name=name + "_sb")
+            nc.sync.dma_start(list_sb[:], src)
+            term_lists.append(list_sb)
+        plain_gates = keep.tile([P, 2, V], F32)
+        nc.sync.dma_start(out=plain_gates[:], in_=gate[2:D].rearrange("d p v -> p d v"))
+
+        ident = keep.tile([P, P], F32)
+        make_identity(nc, ident[:])
+
+        def cast_pair(g, u):
+            pairs = keep.tile([P, T, 2], BF16, name="pairs_%d_%d" % (g, u))
+            last = T // CHUNK - 1
+            share = VECTOR_CAST[2 * g + u]
+            for c in range(T // CHUNK):
+                src = x_raw[g, u, c][:].rearrange("p e t -> p t e")
+                t0 = c * CHUNK
+                if c < last:
+                    nc.scalar.copy(out=pairs[:, t0 : t0 + CHUNK, :], in_=src)
+                else:
+                    nc.vector.tensor_copy(out=pairs[:, t0 : t0 + share, :], in_=src[:, 0:share, :])
+                    nc.scalar.copy(out=pairs[:, t0 + share : t0 + CHUNK, :], in_=src[:, share:CHUNK, :])
+            return pairs[:].rearrange("p t e -> p (t e)").bitcast(U32)
+
+        def gather_pair(window, picked, lo, hi):
+            nc.vector.tensor_copy(out=picked, in_=window.indirect(offs_sb[:, lo // STRIPE : hi // STRIPE]))
+
+        def quantise(codes, values, name):
+            scales = keep.tile(list(codes.shape), U8, align_bytes=64, name="scales_" + name)
+            nc.vector.quantize_mx(out=codes[:].bitcast(FP8X4), scales=scales[:], in_=values)
+            return codes, scales
+
+        def as_values(woven):
+            return woven[:].rearrange("p s u -> p (s u)").bitcast(BF16)
+
+        def product(acc, g, weights, codes, scales):
+            nc.tensor.matmul_mx(
+                out=acc[:],
+                lhsT=weights[0][:].bitcast(FP8X4),
+                lhsT_scale=weights[1][:],
+                rhs=codes.bitcast(FP8X4),
+                rhs_scale=scales,
+                start=(g == 0),
+                stop=(g == PASSES - 1),
+            )
+
+        accs = [psum.tile([P, hi - lo], F32, name="acc_%d" % i) for i, (lo, hi) in enumerate(LAST_SLICES)]
+        half = S // 2
+
+        picked0 = [keep.tile([P, 2, half], U32, name="picked0_%d" % i) for i in range(2)]
+        for u in range(2):
+            window = cast_pair(0, u)
+            for i in range(2):
+                gather_pair(window, picked0[i][:, u, :], i * half, (i + 1) * half)
+        woven0a = keep.tile([P, half, 2], U32, align_bytes=64)
+        nc.vector.tensor_copy(out=woven0a[:].bitcast(I32), in_=picked0[0][:].bitcast(I32).rearrange("p u s -> p s u"))
+
+        window = cast_pair(1, 0)
+        codes0a = reuse.tile([P, half], U32, align_bytes=64, offset=2048)
+        first_a = quantise(codes0a, as_values(woven0a), "0a")
+        woven0b = reuse.tile([P, half, 2], U32, align_bytes=64, offset=0)
+        nc.scalar.copy(out=woven0b[:], in_=picked0[1][:].rearrange("p u s -> p s u"))
+        picked1 = keep.tile([P, 2, S], U32)
+        gather_pair(window, picked1[:, 0, :], 0, S)
+
+        window = cast_pair(1, 1)
+        codes0b = reuse.tile([P, half], U32, align_bytes=64, offset=4096)
+        first_b = quantise(codes0b, as_values(woven0b), "0b")
+        w_bf = []
+        for g in range(PASSES):
+            grouped = keep.tile([P, N, PACK], BF16, align_bytes=64, name="w_bf_%d" % g)
+            nc.scalar.copy(out=grouped[:], in_=w_raw[g][:].rearrange("p j m -> p m j"))
+            w_bf.append(grouped)
+        woven1 = []
+        for i, (lo, hi) in enumerate(LAST_SLICES):
+            gather_pair(window, picked1[:, 1, lo:hi], lo, hi)
+            woven = keep.tile([P, hi - lo, 2], U32, align_bytes=64, name="woven1_%d" % i)
+            nc.scalar.copy(out=woven[:], in_=picked1[:, :, lo:hi].rearrange("p u s -> p s u"))
+            woven1.append(woven)
+        weights = []
+        for g in range(PASSES):
+            w_codes = keep.tile([P, N], U32, align_bytes=64, name="w_codes_%d" % g)
+            weights.append(quantise(w_codes, w_bf[g][:].rearrange("p m j -> p (m j)"), "w%d" % g))
+        for i, (lo, hi) in enumerate(LAST_SLICES):
+            codes, scales = first_a if lo < half else first_b
+            product(accs[i], 0, weights[0], codes[:, lo % half : lo % half + hi - lo], scales[:, lo % half : lo % half + hi - lo])
+        y = keep.tile([P, S], F32)
+        for i, (lo, hi) in enumerate(LAST_SLICES):
+            codes = keep.tile([P, hi - lo], U32, align_bytes=64, name="codes1_%d" % i)
+            codes, scales = quantise(codes, as_values(woven1[i]), "1_%d" % i)
+            product(accs[i], 1, weights[1], codes[:], scales[:])
+            if i < len(LAST_SLICES) - 1:
+                nc.scalar.copy(out=y[:, lo:hi], in_=accs[i][:])
+            else:
+                nc.vector.tensor_copy(out=y[:, lo:hi], in_=accs[i][:])
+
+
+        centre = keep.tile([P, HALVES], F32)
+        spare = keep.tile([P, HALVES, D], F32)
+        for h in range(HALVES):
+            nc.scalar.activation(out=spare[:, h, :], in_=edge[:, :, h], func=COPY, scale=-1.0, bias=1.0 / D, accum_out=centre[:, h : h + 1])
+
+        sums = [psum.tile([P, P], F32, name="sum_%d" % h) for h in range(HALVES)]
+        turned_terms = 3
+        scaled = []
+        for d in range(turned_terms):
+            fetched = keep.tile([P, V], F32, name="fetched_%d" % d)
+            nc.vector.tensor_copy(out=fetched[:], in_=y[:].indirect(term_lists[d][:]))
+            turned = turn.tile([P, HALVES, P], F32, name="turned")
+            for h in range(HALVES):
+                nc.tensor.transpose(turned[:, h, :], fetched[:, h * P : (h + 1) * P], ident[:])
+            weighted = keep.tile([P, HALVES, P], F32, name="weighted_%d" % d)
+            for h in range(HALVES):
+                weight = edge[:, d, h : h + 1] if d < 2 else centre[:, h : h + 1]
+                nc.scalar.activation(out=weighted[:, h, :], in_=turned[:, h, :], func=COPY, scale=weight)
+            scaled.append(weighted)
+        for d in range(turned_terms):
+            for h in range(HALVES):
+                nc.tensor.matmul(sums[h][:], scaled[d][:, h, :], ident[:], start=(d == 0), stop=(d == turned_terms - 1), is_transpose=True)
+
+        products = keep.tile([P, 2, V], F32)
+        for e in range(2):
+            nc.vector.tensor_tensor(products[:, e, :], y[:].indirect(term_lists[turned_terms + e][:]), plain_gates[:, e, :], MULT)
+        both = keep.tile([P, V], F32)
+        nc.vector.tensor_tensor(both[:], products[:, 0, :], products[:, 1, :], ADD)
+        result = keep.tile([P, V], F32)
+        for h in range(HALVES):
+            nc.vector.tensor_tensor(result[:, h * P : (h + 1) * P], sums[h][:], both[:, h * P : (h + 1) * P], ADD)
+        nc.sync.dma_start(out=out, in_=result[:])

@@ -38,6 +38,8 @@ def tile_picked_grand_none_e_kernel(tc, xT, w1, gate, offs, cen, pos1, pos2, pos
         psum = ctx.enter_context(tc.psum_pool(name="psum", bufs=1))
         turn = ctx.enter_context(tc.psum_pool(name="turn", bufs=3))
 
+        gate_rows = keep.tile([P, V], F32)
+        nc.gpsimd.memset(gate_rows[:], 0.0)
         x_rows = xT.rearrange("(g p j) t -> g p j t", g=PASSES, j=PACK)
         x_raw = {}
         offs_sb = lists.tile([P, S // STRIPE], U16)
@@ -52,6 +54,8 @@ def tile_picked_grand_none_e_kernel(tc, xT, w1, gate, offs, cen, pos1, pos2, pos
                     x_raw[g, u, c] = raw
                     if (g, u, c) == (0, 0, 0):
                         nc.sync.dma_start(offs_sb[:], offs)
+                    if (g, u, c) == (0, 0, 1):
+                        nc.sync.dma_start(out=gate_rows[0:D, :], in_=gate[:, 0, :])
 
         w_rows = w1.rearrange("(g p j) m -> g p j m", g=PASSES, j=PACK)
         w_raw = []
@@ -59,10 +63,6 @@ def tile_picked_grand_none_e_kernel(tc, xT, w1, gate, offs, cen, pos1, pos2, pos
             raw = keep.tile([P, PACK, N], F32, name="w_raw_%d" % g)
             nc.sync.dma_start(out=raw[:], in_=w_rows[g])
             w_raw.append(raw)
-        edge = keep.tile([P, D, HALVES], F32)
-        with nc.allow_non_contiguous_dma(reason="one diffusivity a partition"):
-            gate_halves = gate.rearrange("d r (h v) -> (d r h) v", v=P)
-            nc.sync.dma_start(out=edge[:].rearrange("p d h -> p (d h)"), in_=gate_halves[0 : D * P * HALVES : P + 1, :].rearrange("i p -> p i"))
         term_lists = []
         for name, src in (("pos1", pos1), ("pos2", pos2), ("cen", cen), ("pos3", pos3), ("pos4", pos4)):
             list_sb = lists.tile([P, V // STRIPE], U16, name=name + "_sb")
@@ -73,6 +73,18 @@ def tile_picked_grand_none_e_kernel(tc, xT, w1, gate, offs, cen, pos1, pos2, pos
 
         ident = keep.tile([P, P], F32)
         make_identity(nc, ident[:])
+
+        gate_t = turn.tile([P, HALVES, P], F32, name="turned")
+        for h in range(HALVES):
+            nc.tensor.transpose(gate_t[:, h, :], gate_rows[:, h * P : (h + 1) * P], ident[:])
+        edge = keep.tile([P, HALVES, D], F32)
+        centre = keep.tile([P, HALVES], F32)
+        spare = keep.tile([P, HALVES, D], F32)
+
+        def prepare_weights_of_terms():
+            nc.scalar.copy(out=edge[:], in_=gate_t[:, :, 0:D])
+            for h in range(HALVES):
+                nc.scalar.activation(out=spare[:, h, :], in_=gate_t[:, h, 0:D], func=COPY, scale=-1.0, bias=1.0 / D, accum_out=centre[:, h : h + 1])
 
         def cast_pair(g, u):
             pairs = keep.tile([P, T, 2], BF16, name="pairs_%d_%d" % (g, u))
@@ -116,6 +128,8 @@ def tile_picked_grand_none_e_kernel(tc, xT, w1, gate, offs, cen, pos1, pos2, pos
         picked0 = [keep.tile([P, 2, half], U32, name="picked0_%d" % i) for i in range(2)]
         for u in range(2):
             window = cast_pair(0, u)
+            if u == 0:
+                prepare_weights_of_terms()
             for i in range(2):
                 gather_pair(window, picked0[i][:, u, :], i * half, (i + 1) * half)
         woven0a = keep.tile([P, half, 2], U32, align_bytes=64)
@@ -135,7 +149,10 @@ def tile_picked_grand_none_e_kernel(tc, xT, w1, gate, offs, cen, pos1, pos2, pos
         w_bf = []
         for g in range(PASSES):
             grouped = keep.tile([P, N, PACK], BF16, align_bytes=64, name="w_bf_%d" % g)
-            nc.scalar.copy(out=grouped[:], in_=w_raw[g][:].rearrange("p j m -> p m j"))
+            nc.scalar.copy(
+                out=grouped[:].rearrange("p (c i) j -> p c j i", i=4),
+                in_=w_raw[g][:].rearrange("p j (c i) -> p c j i", i=4),
+            )
             w_bf.append(grouped)
         woven1 = []
         for i, (lo, hi) in enumerate(LAST_SLICES):
@@ -161,35 +178,45 @@ def tile_picked_grand_none_e_kernel(tc, xT, w1, gate, offs, cen, pos1, pos2, pos
                 nc.vector.tensor_copy(out=y[:, lo:hi], in_=accs[i][:])
 
 
-        centre = keep.tile([P, HALVES], F32)
-        spare = keep.tile([P, HALVES, D], F32)
-        for h in range(HALVES):
-            nc.scalar.activation(out=spare[:, h, :], in_=edge[:, :, h], func=COPY, scale=-1.0, bias=1.0 / D, accum_out=centre[:, h : h + 1])
-
         sums = [psum.tile([P, P], F32, name="sum_%d" % h) for h in range(HALVES)]
+        cols = P // STRIPE
+        halves = [slice(h * P, (h + 1) * P) for h in range(HALVES)]
         turned_terms = 3
         scaled = []
         for d in range(turned_terms):
             fetched = keep.tile([P, V], F32, name="fetched_%d" % d)
-            nc.vector.tensor_copy(out=fetched[:], in_=y[:].indirect(term_lists[d][:]))
-            turned = turn.tile([P, HALVES, P], F32, name="turned")
-            for h in range(HALVES):
-                nc.tensor.transpose(turned[:, h, :], fetched[:, h * P : (h + 1) * P], ident[:])
             weighted = keep.tile([P, HALVES, P], F32, name="weighted_%d" % d)
-            for h in range(HALVES):
-                weight = edge[:, d, h : h + 1] if d < 2 else centre[:, h : h + 1]
-                nc.scalar.activation(out=weighted[:, h, :], in_=turned[:, h, :], func=COPY, scale=weight)
+            if d < turned_terms - 1:
+                nc.vector.tensor_copy(out=fetched[:], in_=y[:].indirect(term_lists[d][:]))
+                turned = turn.tile([P, HALVES, P], F32, name="turned")
+                for h in range(HALVES):
+                    nc.tensor.transpose(turned[:, h, :], fetched[:, halves[h]], ident[:])
+                for h in range(HALVES):
+                    nc.scalar.activation(out=weighted[:, h, :], in_=turned[:, h, :], func=COPY, scale=edge[:, h, d : d + 1])
+            else:
+                for h in range(HALVES):
+                    nc.vector.tensor_copy(out=fetched[:, halves[h]], in_=y[:].indirect(term_lists[d][:, h * cols : (h + 1) * cols]))
+                    turned = psum.tile([P, P], F32, name="acc_%d" % h)
+                    nc.tensor.transpose(turned[:], fetched[:, halves[h]], ident[:])
+                    nc.scalar.activation(out=weighted[:, h, :], in_=turned[:], func=COPY, scale=centre[:, h : h + 1])
             scaled.append(weighted)
         for d in range(turned_terms):
             for h in range(HALVES):
                 nc.tensor.matmul(sums[h][:], scaled[d][:, h, :], ident[:], start=(d == 0), stop=(d == turned_terms - 1), is_transpose=True)
 
         products = keep.tile([P, 2, V], F32)
-        for e in range(2):
-            nc.vector.tensor_tensor(products[:, e, :], y[:].indirect(term_lists[turned_terms + e][:]), plain_gates[:, e, :], MULT)
-        both = keep.tile([P, V], F32)
-        nc.vector.tensor_tensor(both[:], products[:, 0, :], products[:, 1, :], ADD)
-        result = keep.tile([P, V], F32)
+        nc.vector.tensor_tensor(products[:, 0, :], y[:].indirect(term_lists[turned_terms][:]), plain_gates[:, 0, :], MULT)
         for h in range(HALVES):
-            nc.vector.tensor_tensor(result[:, h * P : (h + 1) * P], sums[h][:], both[:, h * P : (h + 1) * P], ADD)
-        nc.sync.dma_start(out=out, in_=result[:])
+            nc.vector.tensor_tensor(
+                products[:, 1, halves[h]],
+                y[:].indirect(term_lists[turned_terms + 1][:, h * cols : (h + 1) * cols]),
+                plain_gates[:, 1, halves[h]],
+                MULT,
+            )
+        both = keep.tile([P, V], F32)
+        for h in range(HALVES):
+            nc.vector.tensor_tensor(both[:, halves[h]], products[:, 0, halves[h]], products[:, 1, halves[h]], ADD)
+        for h, queue in enumerate((nc.scalar, nc.sync)):
+            result = keep.tile([P, P], F32, name="result_%d" % h)
+            nc.vector.tensor_tensor(result[:], sums[h][:], both[:, halves[h]], ADD)
+            queue.dma_start(out=out[:, halves[h]], in_=result[:])

@@ -16,7 +16,6 @@ FLOPS = 2 * K * N * S
 F32 = mybir.dt.float32
 BF16 = mybir.dt.bfloat16
 U32 = mybir.dt.uint32
-I32 = mybir.dt.int32
 U16 = mybir.dt.uint16
 U8 = mybir.dt.uint8
 FP8X4 = mybir.dt.float8_e4m3fn_x4
@@ -24,9 +23,7 @@ COPY = mybir.ActivationFunctionType.Copy
 ADD = mybir.AluOpType.add
 MULT = mybir.AluOpType.mult
 
-CHUNK = 512
-VECTOR_CAST = (320, 320, 320, 256)
-LAST_SLICES = ((0, 256), (256, 384), (384, 512))
+HALF = S // 2
 
 
 def tile_picked_grand_none_e_kernel(tc, xT, w1, gate, offs, cen, pos1, pos2, pos3, pos4, out):
@@ -36,187 +33,154 @@ def tile_picked_grand_none_e_kernel(tc, xT, w1, gate, offs, cen, pos1, pos2, pos
         keep = ctx.enter_context(tc.tile_pool(name="keep", bufs=1))
         reuse = ctx.enter_context(tc.tile_pool(name="reuse", bufs=1))
         psum = ctx.enter_context(tc.psum_pool(name="psum", bufs=1))
-        turn = ctx.enter_context(tc.psum_pool(name="turn", bufs=3))
 
-        gate_rows = keep.tile([P, V], F32)
-        nc.gpsimd.memset(gate_rows[:], 0.0)
-        x_rows = xT.rearrange("(g p j) t -> g p j t", g=PASSES, j=PACK)
-        x_raw = {}
-        offs_sb = lists.tile([P, S // STRIPE], U16)
-        for g in range(PASSES):
-            for u in range(2):
-                for c in range(T // CHUNK):
-                    if (g, c) == (1, 1):
-                        raw = reuse.tile([P, 2, CHUNK], F32, name="x_raw_reused_%d" % u, align_bytes=64, offset=4096 * u)
-                    else:
-                        raw = keep.tile([P, 2, CHUNK], F32, name="x_raw_%d_%d_%d" % (g, u, c))
-                    nc.sync.dma_start(out=raw[:], in_=x_rows[g, :, 2 * u : 2 * u + 2, c * CHUNK : (c + 1) * CHUNK])
-                    x_raw[g, u, c] = raw
-                    if (g, u, c) == (0, 0, 0):
-                        nc.sync.dma_start(offs_sb[:], offs)
-                    if (g, u, c) == (0, 0, 1):
-                        nc.sync.dma_start(out=gate_rows[0:D, :], in_=gate[:, 0, :])
-
+        gate_rows = keep.tile([P, V + 8], F32)
+        nc.vector.memset(gate_rows[:], 0.0)
+        x_rows = xT.rearrange("(g p j) t -> g j p t", g=PASSES, j=PACK)
         w_rows = w1.rearrange("(g p j) m -> g p j m", g=PASSES, j=PACK)
-        w_raw = []
+        offs_sb = lists.tile([P, S // STRIPE], U16)
+        nc.sync.dma_start(offs_sb[:], offs)
+        rows = {}
         for g in range(PASSES):
-            raw = keep.tile([P, PACK, N], F32, name="w_raw_%d" % g)
-            nc.sync.dma_start(out=raw[:], in_=w_rows[g])
-            w_raw.append(raw)
+            for j in range(PACK):
+                if (g, j) == (PASSES - 1, PACK - 1):
+                    rows[g, j] = reuse.tile([P, T], F32, name="rows_last", align_bytes=64, offset=0)
+                else:
+                    rows[g, j] = keep.tile([P, T], F32, name="rows_%d_%d" % (g, j))
+                nc.sync.dma_start(out=rows[g, j][:], in_=x_rows[g, j])
+                if (g, j) == (0, 0):
+                    nc.sync.dma_start(out=gate_rows[0:D, 0:V], in_=gate[:, 0, :])
+        w_raw = [keep.tile([P, PACK, N], F32, name="w_raw_%d" % g) for g in range(PASSES)]
+        for g in range(PASSES):
+            nc.sync.dma_start(out=w_raw[g][:], in_=w_rows[g])
         term_lists = []
-        for name, src in (("pos1", pos1), ("pos2", pos2), ("cen", cen), ("pos3", pos3), ("pos4", pos4)):
+        for name, src in (("cen", cen), ("pos1", pos1), ("pos2", pos2), ("pos3", pos3), ("pos4", pos4)):
             list_sb = lists.tile([P, V // STRIPE], U16, name=name + "_sb")
             nc.sync.dma_start(list_sb[:], src)
             term_lists.append(list_sb)
-        plain_gates = keep.tile([P, 2, V], F32)
-        nc.sync.dma_start(out=plain_gates[:], in_=gate[2:D].rearrange("d p v -> p d v"))
+        plain_gates = keep.tile([P, D - 1, V], F32)
+        nc.sync.dma_start(out=plain_gates[:], in_=gate[1:D].rearrange("d p v -> p d v"))
 
         ident = keep.tile([P, P], F32)
         make_identity(nc, ident[:])
+        warm = keep.tile([P, 1], F32)
+        nc.scalar.activation(out=warm[:], in_=gate_rows[:, V : V + 1], func=COPY)
 
-        gate_t = turn.tile([P, HALVES, P], F32, name="turned")
-        for h in range(HALVES):
-            nc.tensor.transpose(gate_t[:, h, :], gate_rows[:, h * P : (h + 1) * P], ident[:])
-        edge = keep.tile([P, HALVES, D], F32)
-        centre = keep.tile([P, HALVES], F32)
-        spare = keep.tile([P, HALVES, D], F32)
+        def pick(engine, dst, window, index, lo, hi):
+            src = window[:].indirect(index[:, lo // STRIPE : hi // STRIPE])
+            if engine is nc.vector:
+                nc.vector.tensor_copy(out=dst, in_=src)
+            else:
+                nc.scalar.activation(out=dst, in_=src, func=COPY)
 
-        def prepare_weights_of_terms():
-            nc.scalar.copy(out=edge[:], in_=gate_t[:, :, 0:D])
-            for h in range(HALVES):
-                nc.scalar.activation(out=spare[:, h, :], in_=gate_t[:, h, 0:D], func=COPY, scale=-1.0, bias=1.0 / D, accum_out=centre[:, h : h + 1])
+        def pick_shared(dst, window, split):
+            pick(nc.vector, dst[:, 0:split], window, offs_sb, 0, split)
+            pick(nc.scalar, dst[:, split:S], window, offs_sb, split, S)
 
-        def cast_pair(g, u):
-            pairs = keep.tile([P, T, 2], BF16, name="pairs_%d_%d" % (g, u))
-            last = T // CHUNK - 1
-            share = VECTOR_CAST[2 * g + u]
-            for c in range(T // CHUNK):
-                src = x_raw[g, u, c][:].rearrange("p e t -> p t e")
-                t0 = c * CHUNK
-                if c < last:
-                    nc.scalar.copy(out=pairs[:, t0 : t0 + CHUNK, :], in_=src)
-                else:
-                    nc.vector.tensor_copy(out=pairs[:, t0 : t0 + share, :], in_=src[:, 0:share, :])
-                    nc.scalar.copy(out=pairs[:, t0 + share : t0 + CHUNK, :], in_=src[:, share:CHUNK, :])
-            return pairs[:].rearrange("p t e -> p (t e)").bitcast(U32)
-
-        def gather_pair(window, picked, lo, hi):
-            nc.vector.tensor_copy(out=picked, in_=window.indirect(offs_sb[:, lo // STRIPE : hi // STRIPE]))
-
-        def quantise(codes, values, name):
-            scales = keep.tile(list(codes.shape), U8, align_bytes=64, name="scales_" + name)
-            nc.vector.quantize_mx(out=codes[:].bitcast(FP8X4), scales=scales[:], in_=values)
+        def quantise(values, name):
+            width = values.shape[1]
+            codes = keep.tile([P, width], U32, align_bytes=64, name="codes_" + name)
+            scales = keep.tile([P, width], U8, align_bytes=64, name="scales_" + name)
+            nc.vector.quantize_mx(out=codes[:].bitcast(FP8X4), scales=scales[:], in_=values.rearrange("p s j -> p (s j)"))
             return codes, scales
 
-        def as_values(woven):
-            return woven[:].rearrange("p s u -> p (s u)").bitcast(BF16)
+        def lay_pair(dst, src):
+            nc.vector.tensor_copy(out=dst, in_=src.rearrange("p j s -> p s j"))
 
-        def product(acc, g, weights, codes, scales):
+        gate_t = psum.tile([P, HALVES, P], F32, name="turned_0")
+        for h in range(HALVES):
+            nc.tensor.transpose(gate_t[:, h, :], gate_rows[:, h * P : (h + 1) * P], ident[:])
+        edge = keep.tile([P, HALVES, 1], F32)
+        centre = keep.tile([P, HALVES], F32)
+        spare = keep.tile([P, HALVES, D], F32)
+        nc.scalar.copy(out=edge[:], in_=gate_t[:, :, 0:1])
+        for h in range(HALVES):
+            nc.scalar.activation(out=spare[:, h, :], in_=gate_t[:, h, 0:D], func=COPY, scale=-1.0, bias=1.0 / D, accum_out=centre[:, h : h + 1])
+
+        picked0 = keep.tile([P, PACK, S], BF16)
+        woven0 = keep.tile([P, S, PACK], BF16, align_bytes=64)
+        pick(nc.vector, picked0[:, 0, :], rows[0, 0], offs_sb, 0, S)
+        pick(nc.scalar, picked0[:, 1, :], rows[0, 1], offs_sb, 0, S)
+        pick(nc.scalar, picked0[:, 2, :], rows[0, 2], offs_sb, 0, S)
+        pick_shared(picked0[:, 3, :], rows[0, 3], 320)
+        lay_pair(woven0[:], picked0[:])
+        codes0, scales0 = quantise(woven0[:], "x0")
+
+        picked1 = keep.tile([P, PACK, S], BF16)
+        woven1 = keep.tile([P, S, PACK], BF16, align_bytes=64)
+        pick(nc.scalar, picked1[:, 0, :], rows[1, 0], offs_sb, 0, S)
+        pick(nc.scalar, picked1[:, 1, :], rows[1, 1], offs_sb, 0, S)
+        pick_shared(picked1[:, 2, :], rows[1, 2], HALF)
+        pick(nc.vector, picked1[:, 3, 0:128], rows[1, 3], offs_sb, 0, 128)
+        pick(nc.scalar, picked1[:, 3, 128:HALF], rows[1, 3], offs_sb, 128, HALF)
+        pick(nc.scalar, picked1[:, 3, HALF:S], rows[1, 3], offs_sb, HALF, S)
+        w_bf = []
+        for g in range(PASSES):
+            grouped = reuse.tile([P, N, PACK], BF16, align_bytes=64, name="w_bf_%d" % g, offset=1024 * g)
+            nc.scalar.copy(out=grouped[:].rearrange("p (c i) j -> p c j i", i=4), in_=w_raw[g][:].rearrange("p j (c i) -> p c j i", i=4))
+            w_bf.append(grouped)
+        lay_pair(woven1[:, 0:HALF, :], picked1[:, :, 0:HALF])
+        lay_pair(woven1[:, HALF:S, :], picked1[:, :, HALF:S])
+        first = quantise(woven1[:, 0:HALF, :], "x1a")
+        weights = [quantise(w_bf[0][:], "w0")]
+        weights.append(quantise(w_bf[1][:], "w1"))
+        second = quantise(woven1[:, HALF:S, :], "x1b")
+
+        def product(acc, g, codes, scales):
             nc.tensor.matmul_mx(
                 out=acc[:],
-                lhsT=weights[0][:].bitcast(FP8X4),
-                lhsT_scale=weights[1][:],
+                lhsT=weights[g][0][:].bitcast(FP8X4),
+                lhsT_scale=weights[g][1][:],
                 rhs=codes.bitcast(FP8X4),
                 rhs_scale=scales,
                 start=(g == 0),
                 stop=(g == PASSES - 1),
             )
 
-        accs = [psum.tile([P, hi - lo], F32, name="acc_%d" % i) for i, (lo, hi) in enumerate(LAST_SLICES)]
-        half = S // 2
-
-        picked0 = [keep.tile([P, 2, half], U32, name="picked0_%d" % i) for i in range(2)]
-        for u in range(2):
-            window = cast_pair(0, u)
-            if u == 0:
-                prepare_weights_of_terms()
-            for i in range(2):
-                gather_pair(window, picked0[i][:, u, :], i * half, (i + 1) * half)
-        woven0a = keep.tile([P, half, 2], U32, align_bytes=64)
-        nc.vector.tensor_copy(out=woven0a[:].bitcast(I32), in_=picked0[0][:].bitcast(I32).rearrange("p u s -> p s u"))
-
-        window = cast_pair(1, 0)
-        codes0a = reuse.tile([P, half], U32, align_bytes=64, offset=2048)
-        first_a = quantise(codes0a, as_values(woven0a), "0a")
-        woven0b = reuse.tile([P, half, 2], U32, align_bytes=64, offset=0)
-        nc.scalar.copy(out=woven0b[:], in_=picked0[1][:].rearrange("p u s -> p s u"))
-        picked1 = keep.tile([P, 2, S], U32)
-        gather_pair(window, picked1[:, 0, :], 0, S)
-
-        window = cast_pair(1, 1)
-        codes0b = reuse.tile([P, half], U32, align_bytes=64, offset=4096)
-        first_b = quantise(codes0b, as_values(woven0b), "0b")
-        w_bf = []
-        for g in range(PASSES):
-            grouped = keep.tile([P, N, PACK], BF16, align_bytes=64, name="w_bf_%d" % g)
-            nc.scalar.copy(
-                out=grouped[:].rearrange("p (c i) j -> p c j i", i=4),
-                in_=w_raw[g][:].rearrange("p j (c i) -> p c j i", i=4),
-            )
-            w_bf.append(grouped)
-        woven1 = []
-        for i, (lo, hi) in enumerate(LAST_SLICES):
-            gather_pair(window, picked1[:, 1, lo:hi], lo, hi)
-            woven = keep.tile([P, hi - lo, 2], U32, align_bytes=64, name="woven1_%d" % i)
-            nc.scalar.copy(out=woven[:], in_=picked1[:, :, lo:hi].rearrange("p u s -> p s u"))
-            woven1.append(woven)
-        weights = []
-        for g in range(PASSES):
-            w_codes = keep.tile([P, N], U32, align_bytes=64, name="w_codes_%d" % g)
-            weights.append(quantise(w_codes, w_bf[g][:].rearrange("p m j -> p (m j)"), "w%d" % g))
-        for i, (lo, hi) in enumerate(LAST_SLICES):
-            codes, scales = first_a if lo < half else first_b
-            product(accs[i], 0, weights[0], codes[:, lo % half : lo % half + hi - lo], scales[:, lo % half : lo % half + hi - lo])
+        groups = ((0, HALF), (HALF, HALF + P), (HALF + P, S))
+        accs = [psum.tile([P, hi - lo], F32, name="acc_%d" % i) for i, (lo, hi) in enumerate(groups)]
+        for i, (lo, hi) in enumerate(groups):
+            product(accs[i], 0, codes0[:, lo:hi], scales0[:, lo:hi])
         y = keep.tile([P, S], F32)
-        for i, (lo, hi) in enumerate(LAST_SLICES):
-            codes = keep.tile([P, hi - lo], U32, align_bytes=64, name="codes1_%d" % i)
-            codes, scales = quantise(codes, as_values(woven1[i]), "1_%d" % i)
-            product(accs[i], 1, weights[1], codes[:], scales[:])
-            if i < len(LAST_SLICES) - 1:
-                nc.scalar.copy(out=y[:, lo:hi], in_=accs[i][:])
-            else:
-                nc.vector.tensor_copy(out=y[:, lo:hi], in_=accs[i][:])
+        product(accs[0], 1, first[0][:], first[1][:])
+        nc.scalar.copy(out=y[:, 0:HALF], in_=accs[0][:])
+        product(accs[1], 1, second[0][:, 0:P], second[1][:, 0:P])
+        nc.scalar.copy(out=y[:, HALF : HALF + P], in_=accs[1][:])
+        product(accs[2], 1, second[0][:, P:HALF], second[1][:, P:HALF])
+        nc.vector.tensor_copy(out=y[:, HALF + P : S], in_=accs[2][:])
 
-
-        sums = [psum.tile([P, P], F32, name="sum_%d" % h) for h in range(HALVES)]
-        cols = P // STRIPE
         halves = [slice(h * P, (h + 1) * P) for h in range(HALVES)]
-        turned_terms = 3
-        scaled = []
-        for d in range(turned_terms):
+        factors = (centre, edge[:, :, 0])
+        turned = []
+        for d in range(2):
             fetched = keep.tile([P, V], F32, name="fetched_%d" % d)
-            weighted = keep.tile([P, HALVES, P], F32, name="weighted_%d" % d)
-            if d < turned_terms - 1:
-                nc.vector.tensor_copy(out=fetched[:], in_=y[:].indirect(term_lists[d][:]))
-                turned = turn.tile([P, HALVES, P], F32, name="turned")
-                for h in range(HALVES):
-                    nc.tensor.transpose(turned[:, h, :], fetched[:, halves[h]], ident[:])
-                for h in range(HALVES):
-                    nc.scalar.activation(out=weighted[:, h, :], in_=turned[:, h, :], func=COPY, scale=edge[:, h, d : d + 1])
-            else:
-                for h in range(HALVES):
-                    nc.vector.tensor_copy(out=fetched[:, halves[h]], in_=y[:].indirect(term_lists[d][:, h * cols : (h + 1) * cols]))
-                    turned = psum.tile([P, P], F32, name="acc_%d" % h)
-                    nc.tensor.transpose(turned[:], fetched[:, halves[h]], ident[:])
-                    nc.scalar.activation(out=weighted[:, h, :], in_=turned[:], func=COPY, scale=centre[:, h : h + 1])
-            scaled.append(weighted)
-        for d in range(turned_terms):
+            if d == 0:
+                pick(nc.scalar, fetched[:], y, term_lists[d], 0, V)
+            banks = []
             for h in range(HALVES):
-                nc.tensor.matmul(sums[h][:], scaled[d][:, h, :], ident[:], start=(d == 0), stop=(d == turned_terms - 1), is_transpose=True)
+                if d == 1:
+                    pick(nc.scalar, fetched[:, halves[h]], y, term_lists[d], h * P, (h + 1) * P)
+                bank = psum.tile([P, P], F32, name=("turned_0", "turned_1", "acc_0", "acc_1")[2 * d + h])
+                nc.tensor.transpose(bank[:], fetched[:, halves[h]], ident[:])
+                banks.append(bank)
+            turned.append(banks)
+        weighted = [keep.tile([P, HALVES, P], F32, name="weighted_%d" % d) for d in range(2)]
+        for d in range(2):
+            for h in range(HALVES):
+                nc.scalar.activation(out=weighted[d][:, h, :], in_=turned[d][h][:], func=COPY, scale=factors[d][:, h : h + 1])
+        sums = [psum.tile([P, P], F32, name="sum_%d" % h) for h in range(HALVES)]
+        for d in range(2):
+            for h in range(HALVES):
+                nc.tensor.matmul(sums[h][:], weighted[d][:, h, :], ident[:], start=(d == 0), stop=(d == 1), is_transpose=True)
 
-        products = keep.tile([P, 2, V], F32)
-        nc.vector.tensor_tensor(products[:, 0, :], y[:].indirect(term_lists[turned_terms][:]), plain_gates[:, 0, :], MULT)
-        for h in range(HALVES):
-            nc.vector.tensor_tensor(
-                products[:, 1, halves[h]],
-                y[:].indirect(term_lists[turned_terms + 1][:, h * cols : (h + 1) * cols]),
-                plain_gates[:, 1, halves[h]],
-                MULT,
-            )
-        both = keep.tile([P, V], F32)
-        for h in range(HALVES):
-            nc.vector.tensor_tensor(both[:, halves[h]], products[:, 0, halves[h]], products[:, 1, halves[h]], ADD)
+        products = [keep.tile([P, V], F32, name="product_%d" % d) for d in range(3)]
+        for d in range(3):
+            nc.vector.tensor_tensor(products[d][:], y[:].indirect(term_lists[2 + d][:]), plain_gates[:, d, :], MULT)
+        two = keep.tile([P, V], F32)
+        nc.vector.tensor_tensor(two[:], products[0][:], products[1][:], ADD)
+        three = keep.tile([P, V], F32)
+        nc.vector.tensor_tensor(three[:], two[:], products[2][:], ADD)
         for h, queue in enumerate((nc.scalar, nc.sync)):
             result = keep.tile([P, P], F32, name="result_%d" % h)
-            nc.vector.tensor_tensor(result[:], sums[h][:], both[:, halves[h]], ADD)
+            nc.vector.tensor_tensor(result[:], sums[h][:], three[:, halves[h]], ADD)
             queue.dma_start(out=out[:, halves[h]], in_=result[:])

@@ -58,8 +58,8 @@ def tile_picked_grand_none_e_kernel(tc, xT, w1, gate, offs, cen, pos1, pos2, pos
             list_sb = lists.tile([P, V // STRIPE], U16, name=name + "_sb")
             nc.sync.dma_start(list_sb[:], src)
             term_lists.append(list_sb)
-        plain_gates = keep.tile([P, D - 1, V], F32)
-        nc.sync.dma_start(out=plain_gates[:], in_=gate[1:D].rearrange("d p v -> p d v"))
+        plain_gates = keep.tile([P, 2, V], F32)
+        nc.sync.dma_start(out=plain_gates[:], in_=gate[2:D].rearrange("d p v -> p d v"))
 
         ident = keep.tile([P, P], F32)
         make_identity(nc, ident[:])
@@ -90,10 +90,10 @@ def tile_picked_grand_none_e_kernel(tc, xT, w1, gate, offs, cen, pos1, pos2, pos
         gate_t = psum.tile([P, HALVES, P], F32, name="turned_0")
         for h in range(HALVES):
             nc.tensor.transpose(gate_t[:, h, :], gate_rows[:, h * P : (h + 1) * P], ident[:])
-        edge = keep.tile([P, HALVES, 1], F32)
+        edge = keep.tile([P, HALVES, 2], F32)
         centre = keep.tile([P, HALVES], F32)
         spare = keep.tile([P, HALVES, D], F32)
-        nc.scalar.copy(out=edge[:], in_=gate_t[:, :, 0:1])
+        nc.scalar.copy(out=edge[:], in_=gate_t[:, :, 0:2])
         for h in range(HALVES):
             nc.scalar.activation(out=spare[:, h, :], in_=gate_t[:, h, 0:D], func=COPY, scale=-1.0, bias=1.0 / D, accum_out=centre[:, h : h + 1])
 
@@ -150,37 +150,39 @@ def tile_picked_grand_none_e_kernel(tc, xT, w1, gate, offs, cen, pos1, pos2, pos
         nc.vector.tensor_copy(out=y[:, HALF + P : S], in_=accs[2][:])
 
         halves = [slice(h * P, (h + 1) * P) for h in range(HALVES)]
-        factors = (centre, edge[:, :, 0])
+        factors = (centre, edge[:, :, 0], edge[:, :, 1])
         turned = []
-        for d in range(2):
-            fetched = keep.tile([P, V], F32, name="fetched_%d" % d)
-            if d == 0:
-                pick(nc.scalar, fetched[:], y, term_lists[d], 0, V)
-            banks = []
-            for h in range(HALVES):
-                if d == 1:
-                    pick(nc.scalar, fetched[:, halves[h]], y, term_lists[d], h * P, (h + 1) * P)
-                bank = psum.tile([P, P], F32, name=("turned_0", "turned_1", "acc_0", "acc_1")[2 * d + h])
-                nc.tensor.transpose(bank[:], fetched[:, halves[h]], ident[:])
-                banks.append(bank)
-            turned.append(banks)
-        weighted = [keep.tile([P, HALVES, P], F32, name="weighted_%d" % d) for d in range(2)]
-        for d in range(2):
-            for h in range(HALVES):
-                nc.scalar.activation(out=weighted[d][:, h, :], in_=turned[d][h][:], func=COPY, scale=factors[d][:, h : h + 1])
-        sums = [psum.tile([P, P], F32, name="sum_%d" % h) for h in range(HALVES)]
-        for d in range(2):
-            for h in range(HALVES):
-                nc.tensor.matmul(sums[h][:], weighted[d][:, h, :], ident[:], start=(d == 0), stop=(d == 1), is_transpose=True)
-
-        products = [keep.tile([P, V], F32, name="product_%d" % d) for d in range(3)]
         for d in range(3):
-            nc.vector.tensor_tensor(products[d][:], y[:].indirect(term_lists[2 + d][:]), plain_gates[:, d, :], MULT)
+            fetched = keep.tile([P, V], F32, name="fetched_%d" % d)
+            if d < 2:
+                pick(nc.vector if d == 0 else nc.scalar, fetched[:], y, term_lists[d], 0, V)
+                bank = psum.tile([P, HALVES, P], F32, name="turned_%d" % d)
+                for h in range(HALVES):
+                    nc.tensor.transpose(bank[:, h, :], fetched[:, halves[h]], ident[:])
+                turned.append([bank[:, h, :] for h in range(HALVES)])
+            else:
+                banks = []
+                for h in range(HALVES):
+                    pick(nc.scalar, fetched[:, halves[h]], y, term_lists[d], h * P, (h + 1) * P)
+                    bank = psum.tile([P, P], F32, name="acc_%d" % h)
+                    nc.tensor.transpose(bank[:], fetched[:, halves[h]], ident[:])
+                    banks.append(bank[:])
+                turned.append(banks)
+        weighted = [keep.tile([P, HALVES, P], F32, name="weighted_%d" % d) for d in range(3)]
+        for d in range(3):
+            for h in range(HALVES):
+                nc.scalar.activation(out=weighted[d][:, h, :], in_=turned[d][h], func=COPY, scale=factors[d][:, h : h + 1])
+        sums = [psum.tile([P, P], F32, name="sum_%d" % h) for h in range(HALVES)]
+        for d in range(3):
+            for h in range(HALVES):
+                nc.tensor.matmul(sums[h][:], weighted[d][:, h, :], ident[:], start=(d == 0), stop=(d == 2), is_transpose=True)
+
+        products = [keep.tile([P, V], F32, name="product_%d" % d) for d in range(2)]
+        for d in range(2):
+            nc.vector.tensor_tensor(products[d][:], y[:].indirect(term_lists[3 + d][:]), plain_gates[:, d, :], MULT)
         two = keep.tile([P, V], F32)
         nc.vector.tensor_tensor(two[:], products[0][:], products[1][:], ADD)
-        three = keep.tile([P, V], F32)
-        nc.vector.tensor_tensor(three[:], two[:], products[2][:], ADD)
         for h, queue in enumerate((nc.scalar, nc.sync)):
             result = keep.tile([P, P], F32, name="result_%d" % h)
-            nc.vector.tensor_tensor(result[:], sums[h][:], three[:, halves[h]], ADD)
+            nc.vector.tensor_tensor(result[:], sums[h][:], two[:, halves[h]], ADD)
             queue.dma_start(out=out[:, halves[h]], in_=result[:])

@@ -101,8 +101,8 @@ def tile_picked_grand_none_e_kernel(tc, xT, w1, gate, offs, cen, pos1, pos2, pos
         woven0 = keep.tile([P, S, PACK], BF16, align_bytes=64)
         pick(nc.vector, picked0[:, 0, :], rows[0, 0], offs_sb, 0, S)
         pick(nc.scalar, picked0[:, 1, :], rows[0, 1], offs_sb, 0, S)
-        pick(nc.scalar, picked0[:, 2, :], rows[0, 2], offs_sb, 0, S)
-        pick_shared(picked0[:, 3, :], rows[0, 3], 320)
+        pick(nc.vector, picked0[:, 2, :], rows[0, 2], offs_sb, 0, S)
+        pick_shared(picked0[:, 3, :], rows[0, 3], HALF)
         lay_pair(woven0[:], picked0[:])
         codes0, scales0 = quantise(woven0[:], "x0")
 
@@ -110,7 +110,7 @@ def tile_picked_grand_none_e_kernel(tc, xT, w1, gate, offs, cen, pos1, pos2, pos
         woven1 = keep.tile([P, S, PACK], BF16, align_bytes=64)
         pick(nc.scalar, picked1[:, 0, :], rows[1, 0], offs_sb, 0, S)
         pick(nc.scalar, picked1[:, 1, :], rows[1, 1], offs_sb, 0, S)
-        pick_shared(picked1[:, 2, :], rows[1, 2], HALF)
+        pick(nc.vector, picked1[:, 2, :], rows[1, 2], offs_sb, 0, S)
         pick(nc.vector, picked1[:, 3, 0:128], rows[1, 3], offs_sb, 0, 128)
         pick(nc.scalar, picked1[:, 3, 128:HALF], rows[1, 3], offs_sb, 128, HALF)
         pick(nc.scalar, picked1[:, 3, HALF:S], rows[1, 3], offs_sb, HALF, S)

@@ -39,7 +39,6 @@ def tile_picked_grand_none_e_kernel(tc, xT, w1, gate, offs, cen, pos1, pos2, pos
         x_rows = xT.rearrange("(g p j) t -> g j p t", g=PASSES, j=PACK)
         w_rows = w1.rearrange("(g p j) m -> g p j m", g=PASSES, j=PACK)
         offs_sb = lists.tile([P, S // STRIPE], U16)
-        nc.sync.dma_start(offs_sb[:], offs)
         rows = {}
         for g in range(PASSES):
             for j in range(PACK):
@@ -49,6 +48,7 @@ def tile_picked_grand_none_e_kernel(tc, xT, w1, gate, offs, cen, pos1, pos2, pos
                     rows[g, j] = keep.tile([P, T], F32, name="rows_%d_%d" % (g, j))
                 nc.sync.dma_start(out=rows[g, j][:], in_=x_rows[g, j])
                 if (g, j) == (0, 0):
+                    nc.sync.dma_start(offs_sb[:], offs)
                     nc.sync.dma_start(out=gate_rows[0:D, 0:V], in_=gate[:, 0, :])
         w_raw = [keep.tile([P, PACK, N], F32, name="w_raw_%d" % g) for g in range(PASSES)]
         for g in range(PASSES):
@@ -58,8 +58,8 @@ def tile_picked_grand_none_e_kernel(tc, xT, w1, gate, offs, cen, pos1, pos2, pos
             list_sb = lists.tile([P, V // STRIPE], U16, name=name + "_sb")
             nc.sync.dma_start(list_sb[:], src)
             term_lists.append(list_sb)
-        plain_gates = keep.tile([P, 2, V], F32)
-        nc.sync.dma_start(out=plain_gates[:], in_=gate[2:D].rearrange("d p v -> p d v"))
+        plain_gates = keep.tile([P, D - 1, V], F32)
+        nc.sync.dma_start(out=plain_gates[:], in_=gate[1:D].rearrange("d p v -> p d v"))
 
         ident = keep.tile([P, P], F32)
         make_identity(nc, ident[:])
@@ -85,9 +85,9 @@ def tile_picked_grand_none_e_kernel(tc, xT, w1, gate, offs, cen, pos1, pos2, pos
             return codes, scales
 
         def lay_pair(dst, src):
-            nc.vector.tensor_copy(out=dst, in_=src.rearrange("p j s -> p s j"))
+            nc.vector.tensor_copy(out=dst.rearrange("p (c i) j -> p c j i", i=4), in_=src.rearrange("p j (c i) -> p c j i", i=4))
 
-        gate_t = psum.tile([P, HALVES, P], F32, name="turned_0")
+        gate_t = psum.tile([P, HALVES, P], F32, name="sum_0")
         for h in range(HALVES):
             nc.tensor.transpose(gate_t[:, h, :], gate_rows[:, h * P : (h + 1) * P], ident[:])
         edge = keep.tile([P, HALVES, 2], F32)
@@ -110,7 +110,7 @@ def tile_picked_grand_none_e_kernel(tc, xT, w1, gate, offs, cen, pos1, pos2, pos
         woven1 = keep.tile([P, S, PACK], BF16, align_bytes=64)
         pick(nc.scalar, picked1[:, 0, :], rows[1, 0], offs_sb, 0, S)
         pick(nc.scalar, picked1[:, 1, :], rows[1, 1], offs_sb, 0, S)
-        pick(nc.vector, picked1[:, 2, :], rows[1, 2], offs_sb, 0, S)
+        pick_shared(picked1[:, 2, :], rows[1, 2], 320)
         pick(nc.vector, picked1[:, 3, 0:128], rows[1, 3], offs_sb, 0, 128)
         pick(nc.scalar, picked1[:, 3, 128:HALF], rows[1, 3], offs_sb, 128, HALF)
         pick(nc.scalar, picked1[:, 3, HALF:S], rows[1, 3], offs_sb, HALF, S)
@@ -124,7 +124,8 @@ def tile_picked_grand_none_e_kernel(tc, xT, w1, gate, offs, cen, pos1, pos2, pos
         first = quantise(woven1[:, 0:HALF, :], "x1a")
         weights = [quantise(w_bf[0][:], "w0")]
         weights.append(quantise(w_bf[1][:], "w1"))
-        second = quantise(woven1[:, HALF:S, :], "x1b")
+        second = quantise(woven1[:, HALF : HALF + P, :], "x1b")
+        third = quantise(woven1[:, HALF + P : S, :], "x1c")
 
         def product(acc, g, codes, scales):
             nc.tensor.matmul_mx(
@@ -144,45 +145,46 @@ def tile_picked_grand_none_e_kernel(tc, xT, w1, gate, offs, cen, pos1, pos2, pos
         y = keep.tile([P, S], F32)
         product(accs[0], 1, first[0][:], first[1][:])
         nc.scalar.copy(out=y[:, 0:HALF], in_=accs[0][:])
-        product(accs[1], 1, second[0][:, 0:P], second[1][:, 0:P])
+        product(accs[1], 1, second[0][:], second[1][:])
         nc.scalar.copy(out=y[:, HALF : HALF + P], in_=accs[1][:])
-        product(accs[2], 1, second[0][:, P:HALF], second[1][:, P:HALF])
+        product(accs[2], 1, third[0][:], third[1][:])
         nc.vector.tensor_copy(out=y[:, HALF + P : S], in_=accs[2][:])
 
         halves = [slice(h * P, (h + 1) * P) for h in range(HALVES)]
-        factors = (centre, edge[:, :, 0], edge[:, :, 1])
-        turned = []
-        for d in range(3):
-            fetched = keep.tile([P, V], F32, name="fetched_%d" % d)
-            if d < 2:
-                pick(nc.vector if d == 0 else nc.scalar, fetched[:], y, term_lists[d], 0, V)
-                bank = psum.tile([P, HALVES, P], F32, name="turned_%d" % d)
-                for h in range(HALVES):
-                    nc.tensor.transpose(bank[:, h, :], fetched[:, halves[h]], ident[:])
-                turned.append([bank[:, h, :] for h in range(HALVES)])
-            else:
-                banks = []
-                for h in range(HALVES):
-                    pick(nc.scalar, fetched[:, halves[h]], y, term_lists[d], h * P, (h + 1) * P)
-                    bank = psum.tile([P, P], F32, name="acc_%d" % h)
-                    nc.tensor.transpose(bank[:], fetched[:, halves[h]], ident[:])
-                    banks.append(bank[:])
-                turned.append(banks)
-        weighted = [keep.tile([P, HALVES, P], F32, name="weighted_%d" % d) for d in range(3)]
-        for d in range(3):
-            for h in range(HALVES):
-                nc.scalar.activation(out=weighted[d][:, h, :], in_=turned[d][h], func=COPY, scale=factors[d][:, h : h + 1])
+        cols = P // STRIPE
+        fetched = [keep.tile([P, V], F32, name="fetched_%d" % d) for d in range(2)]
+        extra = keep.tile([P, P], F32)
+        pick(nc.vector, extra[:], y, term_lists[2], 0, P)
+        pick(nc.scalar, fetched[0][:], y, term_lists[0], 0, V)
+        for h in range(HALVES):
+            pick(nc.scalar, fetched[1][:, halves[h]], y, term_lists[1], h * P, (h + 1) * P)
+        steps = [(extra[:], edge[:, 0, 1:2], 0, "acc_2")]
+        steps += [(fetched[0][:, halves[h]], centre[:, h : h + 1], h, "turned_%d" % h) for h in range(HALVES)]
+        steps += [(fetched[1][:, halves[h]], edge[:, h, 0:1], h, "acc_%d" % h) for h in range(HALVES)]
+        banks = []
+        for src, factor, h, bank_name in steps:
+            bank = psum.tile([P, P], F32, name=bank_name)
+            nc.tensor.transpose(bank[:], src, ident[:])
+            banks.append(bank)
+        weighted = []
+        for i, (src, factor, h, bank_name) in enumerate(steps):
+            scaled = keep.tile([P, P], F32, name="weighted_%d" % i)
+            nc.scalar.activation(out=scaled[:], in_=banks[i][:], func=COPY, scale=factor)
+            weighted.append(scaled)
         sums = [psum.tile([P, P], F32, name="sum_%d" % h) for h in range(HALVES)]
-        for d in range(3):
-            for h in range(HALVES):
-                nc.tensor.matmul(sums[h][:], weighted[d][:, h, :], ident[:], start=(d == 0), stop=(d == 2), is_transpose=True)
+        for i, (src, factor, h, bank_name) in enumerate(steps):
+            nc.tensor.matmul(sums[h][:], weighted[i][:], ident[:], start=(i == 2 * h), stop=(i == 3 + h), is_transpose=True)
 
         products = [keep.tile([P, V], F32, name="product_%d" % d) for d in range(2)]
         for d in range(2):
-            nc.vector.tensor_tensor(products[d][:], y[:].indirect(term_lists[3 + d][:]), plain_gates[:, d, :], MULT)
+            nc.vector.tensor_tensor(products[d][:], y[:].indirect(term_lists[3 + d][:]), plain_gates[:, 1 + d, :], MULT)
+        late = keep.tile([P, P], F32)
+        nc.vector.tensor_tensor(late[:], y[:].indirect(term_lists[2][:, cols : 2 * cols]), plain_gates[:, 0, halves[1]], MULT)
         two = keep.tile([P, V], F32)
         nc.vector.tensor_tensor(two[:], products[0][:], products[1][:], ADD)
+        three = keep.tile([P, P], F32)
+        nc.vector.tensor_tensor(three[:], two[:, halves[1]], late[:], ADD)
         for h, queue in enumerate((nc.scalar, nc.sync)):
             result = keep.tile([P, P], F32, name="result_%d" % h)
-            nc.vector.tensor_tensor(result[:], sums[h][:], two[:, halves[h]], ADD)
+            nc.vector.tensor_tensor(result[:], sums[h][:], (two[:, halves[0]], three[:])[h], ADD)
             queue.dma_start(out=out[:, halves[h]], in_=result[:])

@@ -34,7 +34,7 @@ def tile_picked_grand_none_e_kernel(tc, xT, w1, gate, offs, cen, pos1, pos2, pos
         reuse = ctx.enter_context(tc.tile_pool(name="reuse", bufs=1))
         psum = ctx.enter_context(tc.psum_pool(name="psum", bufs=1))
 
-        gate_rows = keep.tile([P, V + 8], F32)
+        gate_rows = keep.tile([P, V], F32)
         nc.vector.memset(gate_rows[:], 0.0)
         x_rows = xT.rearrange("(g p j) t -> g j p t", g=PASSES, j=PACK)
         w_rows = w1.rearrange("(g p j) m -> g p j m", g=PASSES, j=PACK)
@@ -63,8 +63,6 @@ def tile_picked_grand_none_e_kernel(tc, xT, w1, gate, offs, cen, pos1, pos2, pos
 
         ident = keep.tile([P, P], F32)
         make_identity(nc, ident[:])
-        warm = keep.tile([P, 1], F32)
-        nc.scalar.activation(out=warm[:], in_=gate_rows[:, V : V + 1], func=COPY)
 
         def pick(engine, dst, window, index, lo, hi):
             src = window[:].indirect(index[:, lo // STRIPE : hi // STRIPE])
@@ -102,7 +100,7 @@ def tile_picked_grand_none_e_kernel(tc, xT, w1, gate, offs, cen, pos1, pos2, pos
         pick(nc.vector, picked0[:, 0, :], rows[0, 0], offs_sb, 0, S)
         pick(nc.scalar, picked0[:, 1, :], rows[0, 1], offs_sb, 0, S)
         pick(nc.vector, picked0[:, 2, :], rows[0, 2], offs_sb, 0, S)
-        pick_shared(picked0[:, 3, :], rows[0, 3], HALF)
+        pick_shared(picked0[:, 3, :], rows[0, 3], 384)
         lay_pair(woven0[:], picked0[:])
         codes0, scales0 = quantise(woven0[:], "x0")
 

@@ -6,10 +6,16 @@ from concourse.masks import make_identity
 K, T, S, D, V, N = 1024, 1024, 512, 4, 256, 128
 P = 128
 PACK = 4
-K_PASS = P * PACK
-PASSES = K // K_PASS
-HALVES = V // P
+PASSES = K // (P * PACK)
 STRIPE = 16
+HALF = S // 2
+QUARTER = S // 4
+HALVES = V // P
+RUN = 4
+
+VECTOR_SHARE_0_3 = 384
+VECTOR_SHARE_1_2 = 320
+VECTOR_SHARE_POS1 = 64
 
 FLOPS = 2 * K * N * S
 
@@ -23,57 +29,57 @@ COPY = mybir.ActivationFunctionType.Copy
 ADD = mybir.AluOpType.add
 MULT = mybir.AluOpType.mult
 
-HALF = S // 2
-
 
 def tile_picked_grand_none_e_kernel(tc, xT, w1, gate, offs, cen, pos1, pos2, pos3, pos4, out):
     nc = tc.nc
     with ExitStack() as ctx:
         lists = ctx.enter_context(tc.tile_pool(name="lists", bufs=1))
         keep = ctx.enter_context(tc.tile_pool(name="keep", bufs=1))
-        reuse = ctx.enter_context(tc.tile_pool(name="reuse", bufs=1))
         psum = ctx.enter_context(tc.psum_pool(name="psum", bufs=1))
 
         gate_rows = keep.tile([P, V], F32)
         nc.vector.memset(gate_rows[:], 0.0)
-        x_rows = xT.rearrange("(g p j) t -> g j p t", g=PASSES, j=PACK)
+        x_planes = xT.rearrange("(g p j) t -> g j p t", g=PASSES, j=PACK)
         w_rows = w1.rearrange("(g p j) m -> g p j m", g=PASSES, j=PACK)
         offs_sb = lists.tile([P, S // STRIPE], U16)
-        rows = {}
+        planes = {}
         for g in range(PASSES):
             for j in range(PACK):
-                if (g, j) == (PASSES - 1, PACK - 1):
-                    rows[g, j] = reuse.tile([P, T], F32, name="rows_last", align_bytes=64, offset=0)
-                else:
-                    rows[g, j] = keep.tile([P, T], F32, name="rows_%d_%d" % (g, j))
-                nc.sync.dma_start(out=rows[g, j][:], in_=x_rows[g, j])
+                planes[g, j] = keep.tile([P, T], F32, name="plane_%d_%d" % (g, j))
+                nc.sync.dma_start(out=planes[g, j][:], in_=x_planes[g, j])
                 if (g, j) == (0, 0):
                     nc.sync.dma_start(offs_sb[:], offs)
                     nc.sync.dma_start(out=gate_rows[0:D, 0:V], in_=gate[:, 0, :])
         w_raw = [keep.tile([P, PACK, N], F32, name="w_raw_%d" % g) for g in range(PASSES)]
         for g in range(PASSES):
             nc.sync.dma_start(out=w_raw[g][:], in_=w_rows[g])
-        term_lists = []
+        list_sb = {}
         for name, src in (("cen", cen), ("pos1", pos1), ("pos2", pos2), ("pos3", pos3), ("pos4", pos4)):
-            list_sb = lists.tile([P, V // STRIPE], U16, name=name + "_sb")
-            nc.sync.dma_start(list_sb[:], src)
-            term_lists.append(list_sb)
-        plain_gates = keep.tile([P, D - 1, V], F32)
-        nc.sync.dma_start(out=plain_gates[:], in_=gate[1:D].rearrange("d p v -> p d v"))
+            list_sb[name] = lists.tile([P, V // STRIPE], U16, name=name + "_sb")
+            nc.sync.dma_start(list_sb[name][:], src)
+        gate1_upper = keep.tile([P, P], F32)
+        nc.sync.dma_start(out=gate1_upper[:], in_=gate[1, :, P:V])
+        gates23 = keep.tile([P, 2, V], F32)
+        nc.sync.dma_start(out=gates23[:], in_=gate[2:D].rearrange("d p v -> p d v"))
 
         ident = keep.tile([P, P], F32)
         make_identity(nc, ident[:])
 
-        def pick(engine, dst, window, index, lo, hi):
-            src = window[:].indirect(index[:, lo // STRIPE : hi // STRIPE])
-            if engine is nc.vector:
-                nc.vector.tensor_copy(out=dst, in_=src)
-            else:
-                nc.scalar.activation(out=dst, in_=src, func=COPY)
+        def looked_up(window, index, lo, hi):
+            return window[:].indirect(index[:, lo // STRIPE : hi // STRIPE])
 
-        def pick_shared(dst, window, split):
-            pick(nc.vector, dst[:, 0:split], window, offs_sb, 0, split)
-            pick(nc.scalar, dst[:, split:S], window, offs_sb, split, S)
+        def pick(engine, dst, window, index, lo, hi):
+            if engine is nc.vector:
+                nc.vector.tensor_copy(out=dst, in_=looked_up(window, index, lo, hi))
+            else:
+                nc.scalar.activation(out=dst, in_=looked_up(window, index, lo, hi), func=COPY)
+
+        def pick_shared(dst, plane, split):
+            pick(nc.vector, dst[:, 0:split], plane, offs_sb, 0, split)
+            pick(nc.scalar, dst[:, split:S], plane, offs_sb, split, S)
+
+        def weave(copy, dst, src):
+            copy(out=dst.rearrange("p (c i) j -> p c j i", i=RUN), in_=src.rearrange("p j (c i) -> p c j i", i=RUN))
 
         def quantise(values, name):
             width = values.shape[1]
@@ -82,48 +88,44 @@ def tile_picked_grand_none_e_kernel(tc, xT, w1, gate, offs, cen, pos1, pos2, pos
             nc.vector.quantize_mx(out=codes[:].bitcast(FP8X4), scales=scales[:], in_=values.rearrange("p s j -> p (s j)"))
             return codes, scales
 
-        def lay_pair(dst, src):
-            nc.vector.tensor_copy(out=dst.rearrange("p (c i) j -> p c j i", i=4), in_=src.rearrange("p j (c i) -> p c j i", i=4))
-
-        gate_t = psum.tile([P, HALVES, P], F32, name="sum_0")
+        gates_turned = psum.tile([P, HALVES, P], F32, name="sum_0")
         for h in range(HALVES):
-            nc.tensor.transpose(gate_t[:, h, :], gate_rows[:, h * P : (h + 1) * P], ident[:])
-        edge = keep.tile([P, HALVES, 2], F32)
+            nc.tensor.transpose(gates_turned[:, h, :], gate_rows[:, h * P : (h + 1) * P], ident[:])
+        gates01 = keep.tile([P, HALVES, 2], F32)
         centre = keep.tile([P, HALVES], F32)
-        spare = keep.tile([P, HALVES, D], F32)
-        nc.scalar.copy(out=edge[:], in_=gate_t[:, :, 0:2])
+        summands = keep.tile([P, HALVES, D], F32)
+        nc.scalar.copy(out=gates01[:], in_=gates_turned[:, :, 0:2])
         for h in range(HALVES):
-            nc.scalar.activation(out=spare[:, h, :], in_=gate_t[:, h, 0:D], func=COPY, scale=-1.0, bias=1.0 / D, accum_out=centre[:, h : h + 1])
+            nc.scalar.activation(out=summands[:, h, :], in_=gates_turned[:, h, 0:D], func=COPY, scale=-1.0, bias=1.0 / D, accum_out=centre[:, h : h + 1])
 
         picked0 = keep.tile([P, PACK, S], BF16)
         woven0 = keep.tile([P, S, PACK], BF16, align_bytes=64)
-        pick(nc.vector, picked0[:, 0, :], rows[0, 0], offs_sb, 0, S)
-        pick(nc.scalar, picked0[:, 1, :], rows[0, 1], offs_sb, 0, S)
-        pick(nc.vector, picked0[:, 2, :], rows[0, 2], offs_sb, 0, S)
-        pick_shared(picked0[:, 3, :], rows[0, 3], 384)
-        lay_pair(woven0[:], picked0[:])
+        pick(nc.vector, picked0[:, 0, :], planes[0, 0], offs_sb, 0, S)
+        pick(nc.scalar, picked0[:, 1, :], planes[0, 1], offs_sb, 0, S)
+        pick(nc.vector, picked0[:, 2, :], planes[0, 2], offs_sb, 0, S)
+        pick_shared(picked0[:, 3, :], planes[0, 3], VECTOR_SHARE_0_3)
+        weave(nc.vector.tensor_copy, woven0[:], picked0[:])
         codes0, scales0 = quantise(woven0[:], "x0")
 
         picked1 = keep.tile([P, PACK, S], BF16)
         woven1 = keep.tile([P, S, PACK], BF16, align_bytes=64)
-        pick(nc.scalar, picked1[:, 0, :], rows[1, 0], offs_sb, 0, S)
-        pick(nc.scalar, picked1[:, 1, :], rows[1, 1], offs_sb, 0, S)
-        pick_shared(picked1[:, 2, :], rows[1, 2], 320)
-        pick(nc.vector, picked1[:, 3, 0:128], rows[1, 3], offs_sb, 0, 128)
-        pick(nc.scalar, picked1[:, 3, 128:HALF], rows[1, 3], offs_sb, 128, HALF)
-        pick(nc.scalar, picked1[:, 3, HALF:S], rows[1, 3], offs_sb, HALF, S)
-        w_bf = []
+        pick(nc.scalar, picked1[:, 0, :], planes[1, 0], offs_sb, 0, S)
+        pick(nc.scalar, picked1[:, 1, :], planes[1, 1], offs_sb, 0, S)
+        pick_shared(picked1[:, 2, :], planes[1, 2], VECTOR_SHARE_1_2)
+        pick(nc.vector, picked1[:, 3, 0:QUARTER], planes[1, 3], offs_sb, 0, QUARTER)
+        pick(nc.scalar, picked1[:, 3, QUARTER:HALF], planes[1, 3], offs_sb, QUARTER, HALF)
+        pick(nc.scalar, picked1[:, 3, HALF:S], planes[1, 3], offs_sb, HALF, S)
+        w_woven = [keep.tile([P, N, PACK], BF16, align_bytes=64, name="w_woven_%d" % g) for g in range(PASSES)]
         for g in range(PASSES):
-            grouped = reuse.tile([P, N, PACK], BF16, align_bytes=64, name="w_bf_%d" % g, offset=1024 * g)
-            nc.scalar.copy(out=grouped[:].rearrange("p (c i) j -> p c j i", i=4), in_=w_raw[g][:].rearrange("p j (c i) -> p c j i", i=4))
-            w_bf.append(grouped)
-        lay_pair(woven1[:, 0:HALF, :], picked1[:, :, 0:HALF])
-        lay_pair(woven1[:, HALF:S, :], picked1[:, :, HALF:S])
-        first = quantise(woven1[:, 0:HALF, :], "x1a")
-        weights = [quantise(w_bf[0][:], "w0")]
-        weights.append(quantise(w_bf[1][:], "w1"))
-        second = quantise(woven1[:, HALF : HALF + P, :], "x1b")
-        third = quantise(woven1[:, HALF + P : S, :], "x1c")
+            weave(nc.scalar.copy, w_woven[g][:], w_raw[g][:])
+        for lo, hi in ((QUARTER, HALF), (0, QUARTER), (HALF, S)):
+            weave(nc.vector.tensor_copy, woven1[:, lo:hi, :], picked1[:, :, lo:hi])
+        groups = ((0, HALF), (HALF, HALF + QUARTER), (HALF + QUARTER, S))
+        weights = [quantise(w_woven[0][:], "w0")]
+        last_pass = [quantise(woven1[:, 0:HALF, :], "x1_0")]
+        weights.append(quantise(w_woven[1][:], "w1"))
+        for lo, hi in groups[1:]:
+            last_pass.append(quantise(woven1[:, lo:hi, :], "x1_%d" % lo))
 
         def product(acc, g, codes, scales):
             nc.tensor.matmul_mx(
@@ -136,53 +138,57 @@ def tile_picked_grand_none_e_kernel(tc, xT, w1, gate, offs, cen, pos1, pos2, pos
                 stop=(g == PASSES - 1),
             )
 
-        groups = ((0, HALF), (HALF, HALF + P), (HALF + P, S))
         accs = [psum.tile([P, hi - lo], F32, name="acc_%d" % i) for i, (lo, hi) in enumerate(groups)]
-        for i, (lo, hi) in enumerate(groups):
-            product(accs[i], 0, codes0[:, lo:hi], scales0[:, lo:hi])
+        for acc, (lo, hi) in zip(accs, groups):
+            product(acc, 0, codes0[:, lo:hi], scales0[:, lo:hi])
         y = keep.tile([P, S], F32)
-        product(accs[0], 1, first[0][:], first[1][:])
-        nc.scalar.copy(out=y[:, 0:HALF], in_=accs[0][:])
-        product(accs[1], 1, second[0][:], second[1][:])
-        nc.scalar.copy(out=y[:, HALF : HALF + P], in_=accs[1][:])
-        product(accs[2], 1, third[0][:], third[1][:])
-        nc.vector.tensor_copy(out=y[:, HALF + P : S], in_=accs[2][:])
+        copies_out = (nc.scalar.copy, nc.vector.tensor_copy, nc.scalar.copy)
+        for acc, (lo, hi), (codes, scales), copy in zip(accs, groups, last_pass, copies_out):
+            product(acc, 1, codes[:], scales[:])
+            copy(out=y[:, lo:hi], in_=acc[:])
 
         halves = [slice(h * P, (h + 1) * P) for h in range(HALVES)]
-        cols = P // STRIPE
-        fetched = [keep.tile([P, V], F32, name="fetched_%d" % d) for d in range(2)]
-        extra = keep.tile([P, P], F32)
-        pick(nc.vector, extra[:], y, term_lists[2], 0, P)
-        pick(nc.scalar, fetched[0][:], y, term_lists[0], 0, V)
-        for h in range(HALVES):
-            pick(nc.scalar, fetched[1][:, halves[h]], y, term_lists[1], h * P, (h + 1) * P)
-        steps = [(extra[:], edge[:, 0, 1:2], 0, "acc_2")]
-        steps += [(fetched[0][:, halves[h]], centre[:, h : h + 1], h, "turned_%d" % h) for h in range(HALVES)]
-        steps += [(fetched[1][:, halves[h]], edge[:, h, 0:1], h, "acc_%d" % h) for h in range(HALVES)]
-        banks = []
-        for src, factor, h, bank_name in steps:
+        at_cen = keep.tile([P, V], F32)
+        at_pos1 = keep.tile([P, V], F32)
+        at_pos2_lower = keep.tile([P, P], F32)
+        split = V - VECTOR_SHARE_POS1
+        pick(nc.vector, at_pos2_lower[:], y, list_sb["pos2"], 0, P)
+        pick(nc.scalar, at_cen[:], y, list_sb["cen"], 0, V)
+        pick(nc.vector, at_pos1[:, split:V], y, list_sb["pos1"], split, V)
+        pick(nc.scalar, at_pos1[:, 0:P], y, list_sb["pos1"], 0, P)
+        pick(nc.scalar, at_pos1[:, P:split], y, list_sb["pos1"], P, split)
+        turns = [(at_pos2_lower[:], gates01[:, 0, 1:2], 0, "acc_2")]
+        turns += [(at_cen[:, halves[h]], centre[:, h : h + 1], h, "turned_%d" % h) for h in range(HALVES)]
+        turns += [(at_pos1[:, halves[h]], gates01[:, h, 0:1], h, "acc_%d" % h) for h in range(HALVES)]
+        turned = []
+        for values, factor, h, bank_name in turns:
             bank = psum.tile([P, P], F32, name=bank_name)
-            nc.tensor.transpose(bank[:], src, ident[:])
-            banks.append(bank)
-        weighted = []
-        for i, (src, factor, h, bank_name) in enumerate(steps):
-            scaled = keep.tile([P, P], F32, name="weighted_%d" % i)
-            nc.scalar.activation(out=scaled[:], in_=banks[i][:], func=COPY, scale=factor)
-            weighted.append(scaled)
+            nc.tensor.transpose(bank[:], values, ident[:])
+            turned.append(bank)
+        weighed = []
+        for i, (values, factor, h, bank_name) in enumerate(turns):
+            scaled = keep.tile([P, P], F32, name="weighed_%d" % i)
+            nc.scalar.activation(out=scaled[:], in_=turned[i][:], func=COPY, scale=factor)
+            weighed.append(scaled)
         sums = [psum.tile([P, P], F32, name="sum_%d" % h) for h in range(HALVES)]
-        for i, (src, factor, h, bank_name) in enumerate(steps):
-            nc.tensor.matmul(sums[h][:], weighted[i][:], ident[:], start=(i == 2 * h), stop=(i == 3 + h), is_transpose=True)
+        half_of = [turn[2] for turn in turns]
+        for i, h in enumerate(half_of):
+            opens, closes = h not in half_of[:i], h not in half_of[i + 1 :]
+            nc.tensor.matmul(sums[h][:], weighed[i][:], ident[:], start=opens, stop=closes, is_transpose=True)
 
-        products = [keep.tile([P, V], F32, name="product_%d" % d) for d in range(2)]
-        for d in range(2):
-            nc.vector.tensor_tensor(products[d][:], y[:].indirect(term_lists[3 + d][:]), plain_gates[:, 1 + d, :], MULT)
-        late = keep.tile([P, P], F32)
-        nc.vector.tensor_tensor(late[:], y[:].indirect(term_lists[2][:, cols : 2 * cols]), plain_gates[:, 0, halves[1]], MULT)
-        two = keep.tile([P, V], F32)
-        nc.vector.tensor_tensor(two[:], products[0][:], products[1][:], ADD)
-        three = keep.tile([P, P], F32)
-        nc.vector.tensor_tensor(three[:], two[:, halves[1]], late[:], ADD)
+        pos2_upper = keep.tile([P, P], F32)
+        nc.vector.tensor_tensor(pos2_upper[:], looked_up(y, list_sb["pos2"], P, V), gate1_upper[:], MULT)
+        products = []
+        for d, name in enumerate(("pos3", "pos4")):
+            term = keep.tile([P, V], F32, name="term_" + name)
+            nc.vector.tensor_tensor(term[:], looked_up(y, list_sb[name], 0, V), gates23[:, d, :], MULT)
+            products.append(term)
+        upper_part = keep.tile([P, P], F32)
+        nc.vector.tensor_tensor(upper_part[:], pos2_upper[:], products[0][:, halves[1]], ADD)
+        fused = [keep.tile([P, P], F32, name="fused_%d" % h) for h in range(HALVES)]
+        nc.vector.tensor_tensor(fused[0][:], products[0][:, halves[0]], products[1][:, halves[0]], ADD)
+        nc.vector.tensor_tensor(fused[1][:], upper_part[:], products[1][:, halves[1]], ADD)
         for h, queue in enumerate((nc.scalar, nc.sync)):
             result = keep.tile([P, P], F32, name="result_%d" % h)
-            nc.vector.tensor_tensor(result[:], sums[h][:], (two[:, halves[0]], three[:])[h], ADD)
+            nc.vector.tensor_tensor(result[:], sums[h][:], fused[h][:], ADD)
             queue.dma_start(out=out[:, halves[h]], in_=result[:])

@@ -13,8 +13,6 @@ QUARTER = S // 4
 HALVES = V // P
 RUN = 4
 
-VECTOR_SHARE_0_3 = 384
-VECTOR_SHARE_1_2 = 320
 VECTOR_SHARE_POS1 = 64
 
 FLOPS = 2 * K * N * S
@@ -39,17 +37,25 @@ def tile_picked_grand_none_e_kernel(tc, xT, w1, gate, offs, cen, pos1, pos2, pos
 
         gate_rows = keep.tile([P, V], F32)
         nc.vector.memset(gate_rows[:], 0.0)
+        cleared = keep.tile([P, 1], F32)
+        nc.vector.memset(cleared[:], 0.0)
+        warm = keep.tile([P, 1], F32)
+        nc.scalar.activation(out=warm[:], in_=cleared[:], func=COPY)
         x_planes = xT.rearrange("(g p j) t -> g j p t", g=PASSES, j=PACK)
         w_rows = w1.rearrange("(g p j) m -> g p j m", g=PASSES, j=PACK)
         offs_sb = lists.tile([P, S // STRIPE], U16)
+        x_pairs = xT.rearrange("(g p u e) t -> g u p (e t)", g=PASSES, u=2, e=2)
+        pairs = {}
+        for g, u in ((0, 0), (0, 1), (1, 0)):
+            pairs[g, u] = keep.tile([P, 2 * T], F32, name="pair_%d_%d" % (g, u))
+            nc.sync.dma_start(out=pairs[g, u][:], in_=x_pairs[g, u])
+            if (g, u) == (0, 0):
+                nc.sync.dma_start(offs_sb[:], offs)
+                nc.sync.dma_start(out=gate_rows[0:D, 0:V], in_=gate[:, 0, :])
         planes = {}
-        for g in range(PASSES):
-            for j in range(PACK):
-                planes[g, j] = keep.tile([P, T], F32, name="plane_%d_%d" % (g, j))
-                nc.sync.dma_start(out=planes[g, j][:], in_=x_planes[g, j])
-                if (g, j) == (0, 0):
-                    nc.sync.dma_start(offs_sb[:], offs)
-                    nc.sync.dma_start(out=gate_rows[0:D, 0:V], in_=gate[:, 0, :])
+        for j in (2, 3):
+            planes[1, j] = keep.tile([P, T], F32, name="plane_1_%d" % j)
+            nc.sync.dma_start(out=planes[1, j][:], in_=x_planes[1, j])
         w_raw = [keep.tile([P, PACK, N], F32, name="w_raw_%d" % g) for g in range(PASSES)]
         for g in range(PASSES):
             nc.sync.dma_start(out=w_raw[g][:], in_=w_rows[g])
@@ -74,10 +80,6 @@ def tile_picked_grand_none_e_kernel(tc, xT, w1, gate, offs, cen, pos1, pos2, pos
             else:
                 nc.scalar.activation(out=dst, in_=looked_up(window, index, lo, hi), func=COPY)
 
-        def pick_shared(dst, plane, split):
-            pick(nc.vector, dst[:, 0:split], plane, offs_sb, 0, split)
-            pick(nc.scalar, dst[:, split:S], plane, offs_sb, split, S)
-
         def weave(copy, dst, src):
             copy(out=dst.rearrange("p (c i) j -> p c j i", i=RUN), in_=src.rearrange("p j (c i) -> p c j i", i=RUN))
 
@@ -98,28 +100,34 @@ def tile_picked_grand_none_e_kernel(tc, xT, w1, gate, offs, cen, pos1, pos2, pos
         for h in range(HALVES):
             nc.scalar.activation(out=summands[:, h, :], in_=gates_turned[:, h, 0:D], func=COPY, scale=-1.0, bias=1.0 / D, accum_out=centre[:, h : h + 1])
 
-        picked0 = keep.tile([P, PACK, S], BF16)
-        woven0 = keep.tile([P, S, PACK], BF16, align_bytes=64)
-        pick(nc.vector, picked0[:, 0, :], planes[0, 0], offs_sb, 0, S)
-        pick(nc.scalar, picked0[:, 1, :], planes[0, 1], offs_sb, 0, S)
-        pick(nc.vector, picked0[:, 2, :], planes[0, 2], offs_sb, 0, S)
-        pick_shared(picked0[:, 3, :], planes[0, 3], VECTOR_SHARE_0_3)
-        weave(nc.vector.tensor_copy, woven0[:], picked0[:])
-        codes0, scales0 = quantise(woven0[:], "x0")
+        def pick_pair(dst, g, u):
+            for h in range(2):
+                pick(nc.scalar, dst[:, h, 2 * u, :], pairs[g, u], offs_sb, h * HALF, (h + 1) * HALF)
+            nc.vector.tensor_copy(out=dst[:, :, 2 * u + 1, :], in_=pairs[g, u][:, T : 2 * T].indirect(offs_sb[:]))
 
-        picked1 = keep.tile([P, PACK, S], BF16)
-        woven1 = keep.tile([P, S, PACK], BF16, align_bytes=64)
-        pick(nc.scalar, picked1[:, 0, :], planes[1, 0], offs_sb, 0, S)
-        pick(nc.scalar, picked1[:, 1, :], planes[1, 1], offs_sb, 0, S)
-        pick_shared(picked1[:, 2, :], planes[1, 2], VECTOR_SHARE_1_2)
-        pick(nc.vector, picked1[:, 3, 0:QUARTER], planes[1, 3], offs_sb, 0, QUARTER)
-        pick(nc.scalar, picked1[:, 3, QUARTER:HALF], planes[1, 3], offs_sb, QUARTER, HALF)
-        pick(nc.scalar, picked1[:, 3, HALF:S], planes[1, 3], offs_sb, HALF, S)
+        picked0 = keep.tile([P, 2, PACK, HALF], BF16)
+        woven0 = keep.tile([P, S, PACK], BF16, align_bytes=64)
+        for u in range(2):
+            pick_pair(picked0, 0, u)
+        weave(nc.vector.tensor_copy, woven0[:, 0:HALF, :], picked0[:, 0, :, :])
+        weave(nc.vector.tensor_copy, woven0[:, HALF : HALF + QUARTER, :], picked0[:, 1, :, 0:QUARTER])
+        weave(nc.scalar.copy, woven0[:, HALF + QUARTER : S, :], picked0[:, 1, :, QUARTER:HALF])
+        first_pass = [quantise(woven0[:, lo : lo + HALF, :], "x0_%d" % lo) for lo in (0, HALF)]
+
+        picked1 = keep.tile([P, 2, PACK, HALF], BF16)
+        woven1 = woven0
+        pick_pair(picked1, 1, 0)
+        pick(nc.vector, picked1[:, 0, 2, 0:QUARTER], planes[1, 2], offs_sb, 0, QUARTER)
+        pick(nc.scalar, picked1[:, 0, 2, QUARTER:HALF], planes[1, 2], offs_sb, QUARTER, HALF)
+        pick(nc.scalar, picked1[:, 1, 2, :], planes[1, 2], offs_sb, HALF, S)
+        pick(nc.vector, picked1[:, 0, 3, 0:QUARTER], planes[1, 3], offs_sb, 0, QUARTER)
+        pick(nc.scalar, picked1[:, 0, 3, QUARTER:HALF], planes[1, 3], offs_sb, QUARTER, HALF)
+        pick(nc.scalar, picked1[:, 1, 3, :], planes[1, 3], offs_sb, HALF, S)
         w_woven = [keep.tile([P, N, PACK], BF16, align_bytes=64, name="w_woven_%d" % g) for g in range(PASSES)]
         for g in range(PASSES):
             weave(nc.scalar.copy, w_woven[g][:], w_raw[g][:])
         for lo, hi in ((QUARTER, HALF), (0, QUARTER), (HALF, S)):
-            weave(nc.vector.tensor_copy, woven1[:, lo:hi, :], picked1[:, :, lo:hi])
+            weave(nc.vector.tensor_copy, woven1[:, lo:hi, :], picked1[:, lo // HALF, :, lo % HALF : (hi - 1) % HALF + 1])
         groups = ((0, HALF), (HALF, HALF + QUARTER), (HALF + QUARTER, S))
         weights = [quantise(w_woven[0][:], "w0")]
         last_pass = [quantise(woven1[:, 0:HALF, :], "x1_0")]
@@ -140,7 +148,9 @@ def tile_picked_grand_none_e_kernel(tc, xT, w1, gate, offs, cen, pos1, pos2, pos
 
         accs = [psum.tile([P, hi - lo], F32, name="acc_%d" % i) for i, (lo, hi) in enumerate(groups)]
         for acc, (lo, hi) in zip(accs, groups):
-            product(acc, 0, codes0[:, lo:hi], scales0[:, lo:hi])
+            codes, scales = first_pass[lo // HALF]
+            within = slice(lo % HALF, (hi - 1) % HALF + 1)
+            product(acc, 0, codes[:, within], scales[:, within])
         y = keep.tile([P, S], F32)
         copies_out = (nc.scalar.copy, nc.vector.tensor_copy, nc.scalar.copy)
         for acc, (lo, hi), (codes, scales), copy in zip(accs, groups, last_pass, copies_out):

@@ -37,28 +37,19 @@ def tile_picked_grand_none_e_kernel(tc, xT, w1, gate, offs, cen, pos1, pos2, pos
 
         gate_rows = keep.tile([P, V], F32)
         nc.vector.memset(gate_rows[:], 0.0)
-        cleared = keep.tile([P, 1], F32)
-        nc.vector.memset(cleared[:], 0.0)
-        warm = keep.tile([P, 1], F32)
-        nc.scalar.activation(out=warm[:], in_=cleared[:], func=COPY)
-        x_planes = xT.rearrange("(g p j) t -> g j p t", g=PASSES, j=PACK)
+        x_rows = xT.rearrange("(g p j) t -> g p (j t)", g=PASSES, j=PACK)
         w_rows = w1.rearrange("(g p j) m -> g p j m", g=PASSES, j=PACK)
         offs_sb = lists.tile([P, S // STRIPE], U16)
-        x_pairs = xT.rearrange("(g p u e) t -> g u p (e t)", g=PASSES, u=2, e=2)
-        pairs = {}
-        for g, u in ((0, 0), (0, 1), (1, 0)):
-            pairs[g, u] = keep.tile([P, 2 * T], F32, name="pair_%d_%d" % (g, u))
-            nc.sync.dma_start(out=pairs[g, u][:], in_=x_pairs[g, u])
-            if (g, u) == (0, 0):
+        w_raw = [keep.tile([P, PACK, N], F32, name="w_raw_%d" % g) for g in range(PASSES)]
+        nc.sync.dma_start(out=w_raw[0][:], in_=w_rows[0])
+        loaded = {}
+        for g, j, count in ((0, 0, 2), (0, 2, 2), (1, 0, 1), (1, 1, 2), (1, 3, 1)):
+            loaded[g, j] = keep.tile([P, count * T], F32, name="x_%d_%d" % (g, j))
+            nc.sync.dma_start(out=loaded[g, j][:], in_=x_rows[g, :, j * T : (j + count) * T])
+            if (g, j) == (0, 0):
                 nc.sync.dma_start(offs_sb[:], offs)
                 nc.sync.dma_start(out=gate_rows[0:D, 0:V], in_=gate[:, 0, :])
-        planes = {}
-        for j in (2, 3):
-            planes[1, j] = keep.tile([P, T], F32, name="plane_1_%d" % j)
-            nc.sync.dma_start(out=planes[1, j][:], in_=x_planes[1, j])
-        w_raw = [keep.tile([P, PACK, N], F32, name="w_raw_%d" % g) for g in range(PASSES)]
-        for g in range(PASSES):
-            nc.sync.dma_start(out=w_raw[g][:], in_=w_rows[g])
+        nc.sync.dma_start(out=w_raw[1][:], in_=w_rows[1])
         list_sb = {}
         for name, src in (("cen", cen), ("pos1", pos1), ("pos2", pos2), ("pos3", pos3), ("pos4", pos4)):
             list_sb[name] = lists.tile([P, V // STRIPE], U16, name=name + "_sb")
@@ -90,6 +81,10 @@ def tile_picked_grand_none_e_kernel(tc, xT, w1, gate, offs, cen, pos1, pos2, pos
             nc.vector.quantize_mx(out=codes[:].bitcast(FP8X4), scales=scales[:], in_=values.rearrange("p s j -> p (s j)"))
             return codes, scales
 
+        w_woven = [keep.tile([P, N, PACK], BF16, align_bytes=64, name="w_woven_%d" % g) for g in range(PASSES)]
+        weave(nc.scalar.copy, w_woven[0][:], w_raw[0][:])
+        weights = [quantise(w_woven[0][:], "w0")]
+
         gates_turned = psum.tile([P, HALVES, P], F32, name="sum_0")
         for h in range(HALVES):
             nc.tensor.transpose(gates_turned[:, h, :], gate_rows[:, h * P : (h + 1) * P], ident[:])
@@ -100,36 +95,34 @@ def tile_picked_grand_none_e_kernel(tc, xT, w1, gate, offs, cen, pos1, pos2, pos
         for h in range(HALVES):
             nc.scalar.activation(out=summands[:, h, :], in_=gates_turned[:, h, 0:D], func=COPY, scale=-1.0, bias=1.0 / D, accum_out=centre[:, h : h + 1])
 
-        def pick_pair(dst, g, u):
+        def pick_first_row(dst, g, j):
             for h in range(2):
-                pick(nc.scalar, dst[:, h, 2 * u, :], pairs[g, u], offs_sb, h * HALF, (h + 1) * HALF)
-            nc.vector.tensor_copy(out=dst[:, :, 2 * u + 1, :], in_=pairs[g, u][:, T : 2 * T].indirect(offs_sb[:]))
+                pick(nc.scalar, dst[:, h, j, :], loaded[g, j], offs_sb, h * HALF, (h + 1) * HALF)
+
+        def pick_pair(dst, g, j):
+            pick_first_row(dst, g, j)
+            nc.vector.tensor_copy(out=dst[:, :, j + 1, :], in_=loaded[g, j][:, T : 2 * T].indirect(offs_sb[:]))
 
         picked0 = keep.tile([P, 2, PACK, HALF], BF16)
         woven0 = keep.tile([P, S, PACK], BF16, align_bytes=64)
-        for u in range(2):
-            pick_pair(picked0, 0, u)
-        weave(nc.vector.tensor_copy, woven0[:, 0:HALF, :], picked0[:, 0, :, :])
-        weave(nc.vector.tensor_copy, woven0[:, HALF : HALF + QUARTER, :], picked0[:, 1, :, 0:QUARTER])
-        weave(nc.scalar.copy, woven0[:, HALF + QUARTER : S, :], picked0[:, 1, :, QUARTER:HALF])
+        pick_pair(picked0, 0, 0)
+        pick_pair(picked0, 0, 2)
+        for h in range(2):
+            weave(nc.vector.tensor_copy, woven0[:, h * HALF : (h + 1) * HALF, :], picked0[:, h, :, :])
         first_pass = [quantise(woven0[:, lo : lo + HALF, :], "x0_%d" % lo) for lo in (0, HALF)]
 
         picked1 = keep.tile([P, 2, PACK, HALF], BF16)
         woven1 = woven0
-        pick_pair(picked1, 1, 0)
-        pick(nc.vector, picked1[:, 0, 2, 0:QUARTER], planes[1, 2], offs_sb, 0, QUARTER)
-        pick(nc.scalar, picked1[:, 0, 2, QUARTER:HALF], planes[1, 2], offs_sb, QUARTER, HALF)
-        pick(nc.scalar, picked1[:, 1, 2, :], planes[1, 2], offs_sb, HALF, S)
-        pick(nc.vector, picked1[:, 0, 3, 0:QUARTER], planes[1, 3], offs_sb, 0, QUARTER)
-        pick(nc.scalar, picked1[:, 0, 3, QUARTER:HALF], planes[1, 3], offs_sb, QUARTER, HALF)
-        pick(nc.scalar, picked1[:, 1, 3, :], planes[1, 3], offs_sb, HALF, S)
-        w_woven = [keep.tile([P, N, PACK], BF16, align_bytes=64, name="w_woven_%d" % g) for g in range(PASSES)]
-        for g in range(PASSES):
-            weave(nc.scalar.copy, w_woven[g][:], w_raw[g][:])
-        for lo, hi in ((QUARTER, HALF), (0, QUARTER), (HALF, S)):
+        pick_first_row(picked1, 1, 0)
+        pick_pair(picked1, 1, 1)
+        pick(nc.vector, picked1[:, 0, 3, 0:QUARTER], loaded[1, 3], offs_sb, 0, QUARTER)
+        pick(nc.scalar, picked1[:, 0, 3, QUARTER:HALF], loaded[1, 3], offs_sb, QUARTER, HALF)
+        pick(nc.scalar, picked1[:, 1, 3, :], loaded[1, 3], offs_sb, HALF, S)
+        weave(nc.scalar.copy, w_woven[1][:], w_raw[1][:])
+        weave(nc.scalar.copy, woven1[:, HALF + QUARTER : S, :], picked1[:, 1, :, QUARTER:HALF])
+        for lo, hi in ((QUARTER, HALF), (0, QUARTER), (HALF, HALF + QUARTER)):
             weave(nc.vector.tensor_copy, woven1[:, lo:hi, :], picked1[:, lo // HALF, :, lo % HALF : (hi - 1) % HALF + 1])
         groups = ((0, HALF), (HALF, HALF + QUARTER), (HALF + QUARTER, S))
-        weights = [quantise(w_woven[0][:], "w0")]
         last_pass = [quantise(woven1[:, 0:HALF, :], "x1_0")]
         weights.append(quantise(w_woven[1][:], "w1"))
         for lo, hi in groups[1:]:

@@ -111,22 +111,26 @@ def tile_picked_grand_none_e_kernel(tc, xT, w1, gate, offs, cen, pos1, pos2, pos
             weave(nc.vector.tensor_copy, woven0[:, h * HALF : (h + 1) * HALF, :], picked0[:, h, :, :])
         first_pass = [quantise(woven0[:, lo : lo + HALF, :], "x0_%d" % lo) for lo in (0, HALF)]
 
-        picked1 = keep.tile([P, 2, PACK, HALF], BF16)
+        spare = QUARTER * (PACK - 1)
+        staged = keep.tile([P, spare + PACK * S], BF16, align_bytes=64)
+        picked1 = staged[:, spare:].rearrange("p (h j s) -> p h j s", h=2, j=PACK)
+        woven_last = staged[:, 0 : PACK * QUARTER].rearrange("p (s j) -> p s j", j=PACK)
         woven1 = woven0
         pick_first_row(picked1, 1, 0)
         pick_pair(picked1, 1, 1)
         pick(nc.vector, picked1[:, 0, 3, 0:QUARTER], loaded[1, 3], offs_sb, 0, QUARTER)
-        pick(nc.scalar, picked1[:, 0, 3, QUARTER:HALF], loaded[1, 3], offs_sb, QUARTER, HALF)
+        pick(nc.vector, picked1[:, 0, 3, QUARTER:192], loaded[1, 3], offs_sb, QUARTER, 192)
+        pick(nc.scalar, picked1[:, 0, 3, 192:HALF], loaded[1, 3], offs_sb, 192, HALF)
         pick(nc.scalar, picked1[:, 1, 3, :], loaded[1, 3], offs_sb, HALF, S)
         weave(nc.scalar.copy, w_woven[1][:], w_raw[1][:])
-        weave(nc.scalar.copy, woven1[:, HALF + QUARTER : S, :], picked1[:, 1, :, QUARTER:HALF])
-        for lo, hi in ((QUARTER, HALF), (0, QUARTER), (HALF, HALF + QUARTER)):
+        for lo, hi in ((0, QUARTER), (QUARTER, HALF), (HALF, HALF + QUARTER)):
             weave(nc.vector.tensor_copy, woven1[:, lo:hi, :], picked1[:, lo // HALF, :, lo % HALF : (hi - 1) % HALF + 1])
+        weave(nc.scalar.copy, woven_last, picked1[:, 1, :, QUARTER:HALF])
         groups = ((0, HALF), (HALF, HALF + QUARTER), (HALF + QUARTER, S))
         last_pass = [quantise(woven1[:, 0:HALF, :], "x1_0")]
         weights.append(quantise(w_woven[1][:], "w1"))
-        for lo, hi in groups[1:]:
-            last_pass.append(quantise(woven1[:, lo:hi, :], "x1_%d" % lo))
+        last_pass.append(quantise(woven1[:, HALF : HALF + QUARTER, :], "x1_2"))
+        last_pass.append(quantise(woven_last, "x1_3"))
 
         def product(acc, g, codes, scales):
             nc.tensor.matmul_mx(

@@ -14,6 +14,7 @@ HALVES = V // P
 RUN = 4
 
 VECTOR_SHARE_POS1 = 64
+SCALAR_WEAVES = 64
 
 FLOPS = 2 * K * N * S
 
@@ -33,6 +34,7 @@ def tile_picked_grand_none_e_kernel(tc, xT, w1, gate, offs, cen, pos1, pos2, pos
     with ExitStack() as ctx:
         lists = ctx.enter_context(tc.tile_pool(name="lists", bufs=1))
         keep = ctx.enter_context(tc.tile_pool(name="keep", bufs=1))
+        reuse = ctx.enter_context(tc.tile_pool(name="reuse", bufs=1))
         psum = ctx.enter_context(tc.psum_pool(name="psum", bufs=1))
 
         gate_rows = keep.tile([P, V], F32)
@@ -40,8 +42,8 @@ def tile_picked_grand_none_e_kernel(tc, xT, w1, gate, offs, cen, pos1, pos2, pos
         x_rows = xT.rearrange("(g p j) t -> g p (j t)", g=PASSES, j=PACK)
         w_rows = w1.rearrange("(g p j) m -> g p j m", g=PASSES, j=PACK)
         offs_sb = lists.tile([P, S // STRIPE], U16)
-        w_raw = [keep.tile([P, PACK, N], F32, name="w_raw_%d" % g) for g in range(PASSES)]
-        nc.sync.dma_start(out=w_raw[0][:], in_=w_rows[0])
+        w_bytes = PACK * N * 4
+        w_raw = [reuse.tile([P, PACK, N], F32, align_bytes=64, offset=g * w_bytes, name="w_raw_%d" % g) for g in range(PASSES)]
         loaded = {}
         for g, j, count in ((0, 0, 2), (0, 2, 2), (1, 0, 1), (1, 1, 2), (1, 3, 1)):
             loaded[g, j] = keep.tile([P, count * T], F32, name="x_%d_%d" % (g, j))
@@ -49,7 +51,8 @@ def tile_picked_grand_none_e_kernel(tc, xT, w1, gate, offs, cen, pos1, pos2, pos
             if (g, j) == (0, 0):
                 nc.sync.dma_start(offs_sb[:], offs)
                 nc.sync.dma_start(out=gate_rows[0:D, 0:V], in_=gate[:, 0, :])
-        nc.sync.dma_start(out=w_raw[1][:], in_=w_rows[1])
+        for g in range(PASSES):
+            nc.sync.dma_start(out=w_raw[g][:], in_=w_rows[g])
         list_sb = {}
         for name, src in (("cen", cen), ("pos1", pos1), ("pos2", pos2), ("pos3", pos3), ("pos4", pos4)):
             list_sb[name] = lists.tile([P, V // STRIPE], U16, name=name + "_sb")
@@ -74,16 +77,17 @@ def tile_picked_grand_none_e_kernel(tc, xT, w1, gate, offs, cen, pos1, pos2, pos
         def weave(copy, dst, src):
             copy(out=dst.rearrange("p (c i) j -> p c j i", i=RUN), in_=src.rearrange("p j (c i) -> p c j i", i=RUN))
 
-        def quantise(values, name):
+        def quantise(values, name, offset=None):
             width = values.shape[1]
-            codes = keep.tile([P, width], U32, align_bytes=64, name="codes_" + name)
+            if offset is None:
+                codes = keep.tile([P, width], U32, align_bytes=64, name="codes_" + name)
+            else:
+                codes = reuse.tile([P, width], U32, align_bytes=64, offset=offset, name="codes_" + name)
             scales = keep.tile([P, width], U8, align_bytes=64, name="scales_" + name)
             nc.vector.quantize_mx(out=codes[:].bitcast(FP8X4), scales=scales[:], in_=values.rearrange("p s j -> p (s j)"))
             return codes, scales
 
         w_woven = [keep.tile([P, N, PACK], BF16, align_bytes=64, name="w_woven_%d" % g) for g in range(PASSES)]
-        weave(nc.scalar.copy, w_woven[0][:], w_raw[0][:])
-        weights = [quantise(w_woven[0][:], "w0")]
 
         gates_turned = psum.tile([P, HALVES, P], F32, name="sum_0")
         for h in range(HALVES):
@@ -105,32 +109,37 @@ def tile_picked_grand_none_e_kernel(tc, xT, w1, gate, offs, cen, pos1, pos2, pos
 
         picked0 = keep.tile([P, 2, PACK, HALF], BF16)
         woven0 = keep.tile([P, S, PACK], BF16, align_bytes=64)
-        pick_pair(picked0, 0, 0)
-        pick_pair(picked0, 0, 2)
+        for j, share in ((0, HALF), (2, QUARTER)):
+            nc.vector.tensor_copy(out=picked0[:, :, j + 1, :], in_=loaded[0, j][:, T : 2 * T].indirect(offs_sb[:]))
+            pick(nc.vector, picked0[:, 0, j, 0:share], loaded[0, j], offs_sb, 0, share)
+            if share < HALF:
+                pick(nc.scalar, picked0[:, 0, j, share:HALF], loaded[0, j], offs_sb, share, HALF)
+            pick(nc.scalar, picked0[:, 1, j, :], loaded[0, j], offs_sb, HALF, S)
         for h in range(2):
             weave(nc.vector.tensor_copy, woven0[:, h * HALF : (h + 1) * HALF, :], picked0[:, h, :, :])
         first_pass = [quantise(woven0[:, lo : lo + HALF, :], "x0_%d" % lo) for lo in (0, HALF)]
 
-        spare = QUARTER * (PACK - 1)
-        staged = keep.tile([P, spare + PACK * S], BF16, align_bytes=64)
-        picked1 = staged[:, spare:].rearrange("p (h j s) -> p h j s", h=2, j=PACK)
-        woven_last = staged[:, 0 : PACK * QUARTER].rearrange("p (s j) -> p s j", j=PACK)
+        picked1 = keep.tile([P, 2, PACK, HALF], BF16)
         woven1 = woven0
         pick_first_row(picked1, 1, 0)
         pick_pair(picked1, 1, 1)
         pick(nc.vector, picked1[:, 0, 3, 0:QUARTER], loaded[1, 3], offs_sb, 0, QUARTER)
-        pick(nc.vector, picked1[:, 0, 3, QUARTER:192], loaded[1, 3], offs_sb, QUARTER, 192)
-        pick(nc.scalar, picked1[:, 0, 3, 192:HALF], loaded[1, 3], offs_sb, 192, HALF)
+        pick(nc.vector, picked1[:, 0, 3, QUARTER:HALF], loaded[1, 3], offs_sb, QUARTER, HALF)
         pick(nc.scalar, picked1[:, 1, 3, :], loaded[1, 3], offs_sb, HALF, S)
-        weave(nc.scalar.copy, w_woven[1][:], w_raw[1][:])
+        for g in range(PASSES):
+            weave(nc.scalar.copy, w_woven[g][:], w_raw[g][:])
         for lo, hi in ((0, QUARTER), (QUARTER, HALF), (HALF, HALF + QUARTER)):
             weave(nc.vector.tensor_copy, woven1[:, lo:hi, :], picked1[:, lo // HALF, :, lo % HALF : (hi - 1) % HALF + 1])
-        weave(nc.scalar.copy, woven_last, picked1[:, 1, :, QUARTER:HALF])
         groups = ((0, HALF), (HALF, HALF + QUARTER), (HALF + QUARTER, S))
-        last_pass = [quantise(woven1[:, 0:HALF, :], "x1_0")]
+        weights = [quantise(w_woven[0][:], "w0")]
+        last_pass = [quantise(woven1[:, 0:HALF, :], "x1_0", w_bytes // 2)]
+        woven_last = w_woven[0]
+        split = QUARTER - SCALAR_WEAVES
+        weave(nc.vector.tensor_copy, woven_last[:, 0:split, :], picked1[:, 1, :, QUARTER : QUARTER + split])
+        weave(nc.scalar.copy, woven_last[:, split:QUARTER, :], picked1[:, 1, :, QUARTER + split : HALF])
         weights.append(quantise(w_woven[1][:], "w1"))
-        last_pass.append(quantise(woven1[:, HALF : HALF + QUARTER, :], "x1_2"))
-        last_pass.append(quantise(woven_last, "x1_3"))
+        last_pass.append(quantise(woven1[:, HALF : HALF + QUARTER, :], "x1_2", w_bytes))
+        last_pass.append(quantise(woven_last[:], "x1_3", w_bytes + w_bytes // 2))
 
         def product(acc, g, codes, scales):
             nc.tensor.matmul_mx(

@@ -204,7 +204,7 @@ def tile_picked_grand_none_e_kernel(tc, xT, w1, gate, offs, cen, pos1, pos2, pos
         fused = [keep.tile([P, P], F32, name="fused_%d" % h) for h in range(HALVES)]
         nc.vector.tensor_tensor(fused[0][:], products[0][:, halves[0]], products[1][:, halves[0]], ADD)
         nc.vector.tensor_tensor(fused[1][:], upper_part[:], products[1][:, halves[1]], ADD)
-        for h, queue in enumerate((nc.scalar, nc.sync)):
+        for h, queue in enumerate((nc.sync, nc.sync)):
             result = keep.tile([P, P], F32, name="result_%d" % h)
             nc.vector.tensor_tensor(result[:], sums[h][:], fused[h][:], ADD)
             queue.dma_start(out=out[:, halves[h]], in_=result[:])

@@ -15,6 +15,7 @@ RUN = 4
 
 VECTOR_SHARE_POS1 = 64
 SCALAR_WEAVES = 64
+SPREAD = 4
 
 FLOPS = 2 * K * N * S
 
@@ -37,7 +38,7 @@ def tile_picked_grand_none_e_kernel(tc, xT, w1, gate, offs, cen, pos1, pos2, pos
         reuse = ctx.enter_context(tc.tile_pool(name="reuse", bufs=1))
         psum = ctx.enter_context(tc.psum_pool(name="psum", bufs=1))
 
-        gate_rows = keep.tile([P, V], F32)
+        gate_rows = keep.tile([P, P], F32)
         nc.vector.memset(gate_rows[:], 0.0)
         x_rows = xT.rearrange("(g p j) t -> g p (j t)", g=PASSES, j=PACK)
         w_rows = w1.rearrange("(g p j) m -> g p j m", g=PASSES, j=PACK)
@@ -50,7 +51,8 @@ def tile_picked_grand_none_e_kernel(tc, xT, w1, gate, offs, cen, pos1, pos2, pos
             nc.sync.dma_start(out=loaded[g, j][:], in_=x_rows[g, :, j * T : (j + count) * T])
             if (g, j) == (0, 0):
                 nc.sync.dma_start(offs_sb[:], offs)
-                nc.sync.dma_start(out=gate_rows[0:D, 0:V], in_=gate[:, 0, :])
+                half_rows = gate.rearrange("d p (h c) -> (d p h) c", h=HALVES)
+                nc.sync.dma_start(out=gate_rows[0 : D * HALVES * SPREAD : SPREAD, :], in_=half_rows[0 : D * P * HALVES : P + 1, :])
         for g in range(PASSES):
             nc.sync.dma_start(out=w_raw[g][:], in_=w_rows[g])
         list_sb = {}
@@ -89,9 +91,9 @@ def tile_picked_grand_none_e_kernel(tc, xT, w1, gate, offs, cen, pos1, pos2, pos
 
         w_woven = [keep.tile([P, N, PACK], BF16, align_bytes=64, name="w_woven_%d" % g) for g in range(PASSES)]
 
-        gates_turned = psum.tile([P, HALVES, P], F32, name="sum_0")
-        for h in range(HALVES):
-            nc.tensor.transpose(gates_turned[:, h, :], gate_rows[:, h * P : (h + 1) * P], ident[:])
+        gate_bank = psum.tile([P, P], F32, name="sum_0")
+        nc.tensor.transpose(gate_bank[:], gate_rows[:], ident[:])
+        gates_turned = gate_bank[:, 0 : D * HALVES * SPREAD : SPREAD].rearrange("p (d h) -> p h d", h=HALVES)
         gates01 = keep.tile([P, HALVES, 2], F32)
         centre = keep.tile([P, HALVES], F32)
         summands = keep.tile([P, HALVES, D], F32)

@@ -39,7 +39,9 @@ def tile_picked_grand_none_e_kernel(tc, xT, w1, gate, offs, cen, pos1, pos2, pos
         psum = ctx.enter_context(tc.psum_pool(name="psum", bufs=1))
 
         gate_rows = keep.tile([P, P], F32)
-        nc.vector.memset(gate_rows[:], 0.0)
+        zero = keep.tile([P, 1], F32)
+        nc.vector.memset(zero[:], 0.0)
+        nc.scalar.activation(out=gate_rows[:], in_=zero[:].to_broadcast([P, P]), func=COPY)
         x_rows = xT.rearrange("(g p j) t -> g p (j t)", g=PASSES, j=PACK)
         w_rows = w1.rearrange("(g p j) m -> g p j m", g=PASSES, j=PACK)
         offs_sb = lists.tile([P, S // STRIPE], U16)
@@ -111,12 +113,8 @@ def tile_picked_grand_none_e_kernel(tc, xT, w1, gate, offs, cen, pos1, pos2, pos
 
         picked0 = keep.tile([P, 2, PACK, HALF], BF16)
         woven0 = keep.tile([P, S, PACK], BF16, align_bytes=64)
-        for j, share in ((0, HALF), (2, QUARTER)):
-            nc.vector.tensor_copy(out=picked0[:, :, j + 1, :], in_=loaded[0, j][:, T : 2 * T].indirect(offs_sb[:]))
-            pick(nc.vector, picked0[:, 0, j, 0:share], loaded[0, j], offs_sb, 0, share)
-            if share < HALF:
-                pick(nc.scalar, picked0[:, 0, j, share:HALF], loaded[0, j], offs_sb, share, HALF)
-            pick(nc.scalar, picked0[:, 1, j, :], loaded[0, j], offs_sb, HALF, S)
+        for j in (0, 2):
+            pick_pair(picked0, 0, j)
         for h in range(2):
             weave(nc.vector.tensor_copy, woven0[:, h * HALF : (h + 1) * HALF, :], picked0[:, h, :, :])
         first_pass = [quantise(woven0[:, lo : lo + HALF, :], "x0_%d" % lo) for lo in (0, HALF)]

@@ -16,6 +16,7 @@ RUN = 4
 VECTOR_SHARE_POS1 = 64
 SCALAR_WEAVES = 64
 SPREAD = 4
+VECTOR_SHARE_1_2 = 384
 
 FLOPS = 2 * K * N * S
 
@@ -48,7 +49,7 @@ def tile_picked_grand_none_e_kernel(tc, xT, w1, gate, offs, cen, pos1, pos2, pos
         w_bytes = PACK * N * 4
         w_raw = [reuse.tile([P, PACK, N], F32, align_bytes=64, offset=g * w_bytes, name="w_raw_%d" % g) for g in range(PASSES)]
         loaded = {}
-        for g, j, count in ((0, 0, 2), (0, 2, 2), (1, 0, 1), (1, 1, 2), (1, 3, 1)):
+        for g, j, count in ((0, 0, 2), (0, 2, 2), (1, 0, 1), (1, 1, 1), (1, 2, 1), (1, 3, 1)):
             loaded[g, j] = keep.tile([P, count * T], F32, name="x_%d_%d" % (g, j))
             nc.sync.dma_start(out=loaded[g, j][:], in_=x_rows[g, :, j * T : (j + count) * T])
             if (g, j) == (0, 0):
@@ -119,24 +120,30 @@ def tile_picked_grand_none_e_kernel(tc, xT, w1, gate, offs, cen, pos1, pos2, pos
             weave(nc.vector.tensor_copy, woven0[:, h * HALF : (h + 1) * HALF, :], picked0[:, h, :, :])
         first_pass = [quantise(woven0[:, lo : lo + HALF, :], "x0_%d" % lo) for lo in (0, HALF)]
 
-        picked1 = keep.tile([P, 2, PACK, HALF], BF16)
+        picked1 = keep.tile([P, PACK, S], BF16)
         woven1 = woven0
-        pick_first_row(picked1, 1, 0)
-        pick_pair(picked1, 1, 1)
-        pick(nc.vector, picked1[:, 0, 3, 0:QUARTER], loaded[1, 3], offs_sb, 0, QUARTER)
-        pick(nc.vector, picked1[:, 0, 3, QUARTER:HALF], loaded[1, 3], offs_sb, QUARTER, HALF)
-        pick(nc.scalar, picked1[:, 1, 3, :], loaded[1, 3], offs_sb, HALF, S)
+
+        def pick_plane(engine, j, lo, hi):
+            pick(engine, picked1[:, j, lo:hi], loaded[1, j], offs_sb, lo, hi)
+
+        pick_plane(nc.scalar, 0, 0, S)
+        pick_plane(nc.scalar, 1, 0, S)
+        pick_plane(nc.vector, 2, 0, VECTOR_SHARE_1_2)
+        pick_plane(nc.scalar, 2, VECTOR_SHARE_1_2, S)
+        pick_plane(nc.vector, 3, 0, QUARTER)
+        pick_plane(nc.vector, 3, QUARTER, HALF)
+        pick_plane(nc.scalar, 3, HALF, S)
         for g in range(PASSES):
             weave(nc.scalar.copy, w_woven[g][:], w_raw[g][:])
         for lo, hi in ((0, QUARTER), (QUARTER, HALF), (HALF, HALF + QUARTER)):
-            weave(nc.vector.tensor_copy, woven1[:, lo:hi, :], picked1[:, lo // HALF, :, lo % HALF : (hi - 1) % HALF + 1])
+            weave(nc.vector.tensor_copy, woven1[:, lo:hi, :], picked1[:, :, lo:hi])
         groups = ((0, HALF), (HALF, HALF + QUARTER), (HALF + QUARTER, S))
         weights = [quantise(w_woven[0][:], "w0")]
         last_pass = [quantise(woven1[:, 0:HALF, :], "x1_0", w_bytes // 2)]
         woven_last = w_woven[0]
         split = QUARTER - SCALAR_WEAVES
-        weave(nc.vector.tensor_copy, woven_last[:, 0:split, :], picked1[:, 1, :, QUARTER : QUARTER + split])
-        weave(nc.scalar.copy, woven_last[:, split:QUARTER, :], picked1[:, 1, :, QUARTER + split : HALF])
+        weave(nc.vector.tensor_copy, woven_last[:, 0:split, :], picked1[:, :, S - QUARTER : S - QUARTER + split])
+        weave(nc.scalar.copy, woven_last[:, split:QUARTER, :], picked1[:, :, S - QUARTER + split : S])
         weights.append(quantise(w_woven[1][:], "w1"))
         last_pass.append(quantise(woven1[:, HALF : HALF + QUARTER, :], "x1_2", w_bytes))
         last_pass.append(quantise(woven_last[:], "x1_3", w_bytes + w_bytes // 2))
@@ -170,9 +177,8 @@ def tile_picked_grand_none_e_kernel(tc, xT, w1, gate, offs, cen, pos1, pos2, pos
         split = V - VECTOR_SHARE_POS1
         pick(nc.vector, at_pos2_lower[:], y, list_sb["pos2"], 0, P)
         pick(nc.scalar, at_cen[:], y, list_sb["cen"], 0, V)
-        pick(nc.vector, at_pos1[:, split:V], y, list_sb["pos1"], split, V)
         pick(nc.scalar, at_pos1[:, 0:P], y, list_sb["pos1"], 0, P)
-        pick(nc.scalar, at_pos1[:, P:split], y, list_sb["pos1"], P, split)
+        pick(nc.scalar, at_pos1[:, P:V], y, list_sb["pos1"], P, V)
         turns = [(at_pos2_lower[:], gates01[:, 0, 1:2], 0, "acc_2")]
         turns += [(at_cen[:, halves[h]], centre[:, h : h + 1], h, "turned_%d" % h) for h in range(HALVES)]
         turns += [(at_pos1[:, halves[h]], gates01[:, h, 0:1], h, "acc_%d" % h) for h in range(HALVES)]

@@ -1,7 +1,6 @@
 from contextlib import ExitStack
 
 import concourse.mybir as mybir
-from concourse.masks import make_identity
 
 K, T, S, D, V, N = 1024, 1024, 512, 4, 256, 128
 P = 128
@@ -68,7 +67,14 @@ def tile_picked_grand_none_e_kernel(tc, xT, w1, gate, offs, cen, pos1, pos2, pos
         nc.sync.dma_start(out=gates23[:], in_=gate[2:D].rearrange("d p v -> p d v"))
 
         ident = keep.tile([P, P], F32)
-        make_identity(nc, ident[:])
+        ones = keep.tile([P, P], F32)
+        nc.vector.memset(ones[:], 1.0)
+        column = keep.tile([P, P], F32, align_bytes=64)
+        nc.vector.tensor_tensor_scan(column[:], ones[:], ones[:], -1.0, MULT, ADD)
+        blocks = keep.tile([P, P], F32, align_bytes=64)
+        nc.vector.transpose(blocks[:], column[:])
+        for q in range(0, P, 32):
+            nc.vector.tensor_scalar(ident[q : q + 32, :], column[q : q + 32, :], blocks[q : q + 32, q : q + 1], None, mybir.AluOpType.is_equal)
 
         def looked_up(window, index, lo, hi):
             return window[:].indirect(index[:, lo // STRIPE : hi // STRIPE])

@@ -53,6 +53,7 @@ def tile_picked_grand_none_e_kernel(tc, xT, w1, gate, offs, cen, pos1, pos2, pos
             nc.sync.dma_start(out=loaded[g, j][:], in_=x_rows[g, :, j * T : (j + count) * T])
             if (g, j) == (0, 0):
                 nc.sync.dma_start(offs_sb[:], offs)
+            if (g, j) == (0, 2):
                 half_rows = gate.rearrange("d p (h c) -> (d p h) c", h=HALVES)
                 nc.sync.dma_start(out=gate_rows[0 : D * HALVES * SPREAD : SPREAD, :], in_=half_rows[0 : D * P * HALVES : P + 1, :])
         for g in range(PASSES):

@@ -12,7 +12,6 @@ QUARTER = S // 4
 HALVES = V // P
 RUN = 4
 
-VECTOR_SHARE_POS1 = 64
 SCALAR_WEAVES = 64
 SPREAD = 4
 VECTOR_SHARE_1_2 = 384
@@ -48,8 +47,13 @@ def tile_picked_grand_none_e_kernel(tc, xT, w1, gate, offs, cen, pos1, pos2, pos
         w_bytes = PACK * N * 4
         w_raw = [reuse.tile([P, PACK, N], F32, align_bytes=64, offset=g * w_bytes, name="w_raw_%d" % g) for g in range(PASSES)]
         loaded = {}
+        on_first_pair = {(0, 0): 0, (1, 2): 0, (1, 3): 1}
         for g, j, count in ((0, 0, 2), (0, 2, 2), (1, 0, 1), (1, 1, 1), (1, 2, 1), (1, 3, 1)):
-            loaded[g, j] = keep.tile([P, count * T], F32, name="x_%d_%d" % (g, j))
+            if (g, j) in on_first_pair:
+                at = PASSES * w_bytes + on_first_pair[g, j] * T * 4
+                loaded[g, j] = reuse.tile([P, count * T], F32, align_bytes=64, offset=at, name="x_%d_%d" % (g, j))
+            else:
+                loaded[g, j] = keep.tile([P, count * T], F32, name="x_%d_%d" % (g, j))
             nc.sync.dma_start(out=loaded[g, j][:], in_=x_rows[g, :, j * T : (j + count) * T])
             if (g, j) == (0, 0):
                 nc.sync.dma_start(offs_sb[:], offs)
@@ -181,7 +185,6 @@ def tile_picked_grand_none_e_kernel(tc, xT, w1, gate, offs, cen, pos1, pos2, pos
         at_cen = keep.tile([P, V], F32)
         at_pos1 = keep.tile([P, V], F32)
         at_pos2_lower = keep.tile([P, P], F32)
-        split = V - VECTOR_SHARE_POS1
         pick(nc.vector, at_pos2_lower[:], y, list_sb["pos2"], 0, P)
         pick(nc.scalar, at_cen[:], y, list_sb["cen"], 0, V)
         pick(nc.scalar, at_pos1[:, 0:P], y, list_sb["pos1"], 0, P)

@@ -37,7 +37,7 @@ def tile_picked_grand_none_e_kernel(tc, xT, w1, gate, offs, cen, pos1, pos2, pos
         reuse = ctx.enter_context(tc.tile_pool(name="reuse", bufs=1))
         psum = ctx.enter_context(tc.psum_pool(name="psum", bufs=1))
 
-        gate_rows = keep.tile([P, P], F32)
+        gate_rows = reuse.tile([P, P], F32, align_bytes=64, offset=4 * T * 4)
         zero = keep.tile([P, 1], F32)
         nc.vector.memset(zero[:], 0.0)
         nc.scalar.activation(out=gate_rows[:], in_=zero[:].to_broadcast([P, P]), func=COPY)
@@ -45,12 +45,13 @@ def tile_picked_grand_none_e_kernel(tc, xT, w1, gate, offs, cen, pos1, pos2, pos
         w_rows = w1.rearrange("(g p j) m -> g p j m", g=PASSES, j=PACK)
         offs_sb = lists.tile([P, S // STRIPE], U16)
         w_bytes = PACK * N * 4
-        w_raw = [reuse.tile([P, PACK, N], F32, align_bytes=64, offset=g * w_bytes, name="w_raw_%d" % g) for g in range(PASSES)]
+        w_at = 2 * T * 4
+        w_raw = [reuse.tile([P, PACK, N], F32, align_bytes=64, offset=w_at + g * w_bytes, name="w_raw_%d" % g) for g in range(PASSES)]
         loaded = {}
-        on_first_pair = {(0, 0): 0, (1, 2): 0, (1, 3): 1}
+        on_first_pair = {(0, 0): 0, (0, 2): 2, (1, 2): 0, (1, 3): 4}
         for g, j, count in ((0, 0, 2), (0, 2, 2), (1, 0, 1), (1, 1, 1), (1, 2, 1), (1, 3, 1)):
             if (g, j) in on_first_pair:
-                at = PASSES * w_bytes + on_first_pair[g, j] * T * 4
+                at = on_first_pair[g, j] * T * 4
                 loaded[g, j] = reuse.tile([P, count * T], F32, align_bytes=64, offset=at, name="x_%d_%d" % (g, j))
             else:
                 loaded[g, j] = keep.tile([P, count * T], F32, name="x_%d_%d" % (g, j))
@@ -150,14 +151,14 @@ def tile_picked_grand_none_e_kernel(tc, xT, w1, gate, offs, cen, pos1, pos2, pos
             weave(nc.vector.tensor_copy, woven1[:, lo:hi, :], picked1[:, :, lo:hi])
         groups = ((0, HALF), (HALF, HALF + QUARTER), (HALF + QUARTER, S))
         weights = [quantise(w_woven[0][:], "w0")]
-        last_pass = [quantise(woven1[:, 0:HALF, :], "x1_0", w_bytes // 2)]
+        last_pass = [quantise(woven1[:, 0:HALF, :], "x1_0", w_at + w_bytes // 2)]
         woven_last = w_woven[0]
         split = QUARTER - SCALAR_WEAVES
         weave(nc.vector.tensor_copy, woven_last[:, 0:split, :], picked1[:, :, S - QUARTER : S - QUARTER + split])
         weave(nc.scalar.copy, woven_last[:, split:QUARTER, :], picked1[:, :, S - QUARTER + split : S])
         weights.append(quantise(w_woven[1][:], "w1"))
-        last_pass.append(quantise(woven1[:, HALF : HALF + QUARTER, :], "x1_2", w_bytes))
-        last_pass.append(quantise(woven_last[:], "x1_3", w_bytes + w_bytes // 2))
+        last_pass.append(quantise(woven1[:, HALF : HALF + QUARTER, :], "x1_2", w_at + w_bytes))
+        last_pass.append(quantise(woven_last[:], "x1_3", w_at + w_bytes + w_bytes // 2))
 
         def product(acc, g, codes, scales):
             nc.tensor.matmul_mx(

@@ -48,7 +48,7 @@ def tile_picked_grand_none_e_kernel(tc, xT, w1, gate, offs, cen, pos1, pos2, pos
         w_at = 2 * T * 4
         w_raw = [reuse.tile([P, PACK, N], F32, align_bytes=64, offset=w_at + g * w_bytes, name="w_raw_%d" % g) for g in range(PASSES)]
         loaded = {}
-        on_first_pair = {(0, 0): 0, (0, 2): 2, (1, 2): 0, (1, 3): 4}
+        on_first_pair = {(0, 0): 0, (0, 2): 2, (1, 1): 4, (1, 2): 0, (1, 3): 1}
         for g, j, count in ((0, 0, 2), (0, 2, 2), (1, 0, 1), (1, 1, 1), (1, 2, 1), (1, 3, 1)):
             if (g, j) in on_first_pair:
                 at = on_first_pair[g, j] * T * 4
@@ -58,7 +58,6 @@ def tile_picked_grand_none_e_kernel(tc, xT, w1, gate, offs, cen, pos1, pos2, pos
             nc.sync.dma_start(out=loaded[g, j][:], in_=x_rows[g, :, j * T : (j + count) * T])
             if (g, j) == (0, 0):
                 nc.sync.dma_start(offs_sb[:], offs)
-            if (g, j) == (0, 2):
                 half_rows = gate.rearrange("d p (h c) -> (d p h) c", h=HALVES)
                 nc.sync.dma_start(out=gate_rows[0 : D * HALVES * SPREAD : SPREAD, :], in_=half_rows[0 : D * P * HALVES : P + 1, :])
         for g in range(PASSES):

from contextlib import ExitStack

import concourse.mybir as mybir

K, T, S, D, V, N = 1024, 1024, 512, 4, 256, 128
P = 128
PACK = 4
PASSES = K // (P * PACK)
STRIPE = 16
HALF = S // 2
QUARTER = S // 4
HALVES = V // P
RUN = 4

SCALAR_WEAVES = 64
SPREAD = 4
VECTOR_SHARE_1_2 = 384

FLOPS = 2 * K * N * S

F32 = mybir.dt.float32
BF16 = mybir.dt.bfloat16
U32 = mybir.dt.uint32
U16 = mybir.dt.uint16
U8 = mybir.dt.uint8
FP8X4 = mybir.dt.float8_e4m3fn_x4
COPY = mybir.ActivationFunctionType.Copy
ADD = mybir.AluOpType.add
MULT = mybir.AluOpType.mult


def tile_picked_grand_none_e_kernel(tc, xT, w1, gate, offs, cen, pos1, pos2, pos3, pos4, out):
    nc = tc.nc
    with ExitStack() as ctx:
        lists = ctx.enter_context(tc.tile_pool(name="lists", bufs=1))
        keep = ctx.enter_context(tc.tile_pool(name="keep", bufs=1))
        reuse = ctx.enter_context(tc.tile_pool(name="reuse", bufs=1))
        psum = ctx.enter_context(tc.psum_pool(name="psum", bufs=1))

        gate_rows = reuse.tile([P, P], F32, align_bytes=64, offset=4 * T * 4)
        zero = keep.tile([P, 1], F32)
        nc.vector.memset(zero[:], 0.0)
        nc.scalar.activation(out=gate_rows[:], in_=zero[:].to_broadcast([P, P]), func=COPY)
        x_rows = xT.rearrange("(g p j) t -> g p (j t)", g=PASSES, j=PACK)
        w_rows = w1.rearrange("(g p j) m -> g p j m", g=PASSES, j=PACK)
        offs_sb = lists.tile([P, S // STRIPE], U16)
        w_bytes = PACK * N * 4
        w_at = 2 * T * 4
        w_raw = [reuse.tile([P, PACK, N], F32, align_bytes=64, offset=w_at + g * w_bytes, name="w_raw_%d" % g) for g in range(PASSES)]
        loaded = {}
        on_first_pair = {(0, 0): 0, (0, 2): 2, (1, 1): 4, (1, 2): 0, (1, 3): 1}
        for g, j, count in ((0, 0, 2), (0, 2, 2), (1, 0, 1), (1, 1, 1), (1, 2, 1), (1, 3, 1)):
            if (g, j) in on_first_pair:
                at = on_first_pair[g, j] * T * 4
                loaded[g, j] = reuse.tile([P, count * T], F32, align_bytes=64, offset=at, name="x_%d_%d" % (g, j))
            else:
                loaded[g, j] = keep.tile([P, count * T], F32, name="x_%d_%d" % (g, j))
            nc.sync.dma_start(out=loaded[g, j][:], in_=x_rows[g, :, j * T : (j + count) * T])
            if (g, j) == (0, 0):
                nc.sync.dma_start(offs_sb[:], offs)
                half_rows = gate.rearrange("d p (h c) -> (d p h) c", h=HALVES)
                nc.sync.dma_start(out=gate_rows[0 : D * HALVES * SPREAD : SPREAD, :], in_=half_rows[0 : D * P * HALVES : P + 1, :])
        for g in range(PASSES):
            nc.sync.dma_start(out=w_raw[g][:], in_=w_rows[g])
        list_sb = {}
        for name, src in (("cen", cen), ("pos1", pos1), ("pos2", pos2), ("pos3", pos3), ("pos4", pos4)):
            list_sb[name] = lists.tile([P, V // STRIPE], U16, name=name + "_sb")
            nc.sync.dma_start(list_sb[name][:], src)
        gate1_upper = keep.tile([P, P], F32)
        nc.sync.dma_start(out=gate1_upper[:], in_=gate[1, :, P:V])
        gates23 = keep.tile([P, 2, V], F32)
        nc.sync.dma_start(out=gates23[:], in_=gate[2:D].rearrange("d p v -> p d v"))

        ident = keep.tile([P, P], F32)
        ones = keep.tile([P, P], F32)
        nc.vector.memset(ones[:], 1.0)
        column = keep.tile([P, P], F32, align_bytes=64)
        nc.vector.tensor_tensor_scan(column[:], ones[:], ones[:], -1.0, MULT, ADD)
        blocks = keep.tile([P, P], F32, align_bytes=64)
        nc.vector.transpose(blocks[:], column[:])
        for q in range(0, P, 32):
            nc.vector.tensor_scalar(ident[q : q + 32, :], column[q : q + 32, :], blocks[q : q + 32, q : q + 1], None, mybir.AluOpType.is_equal)

        def looked_up(window, index, lo, hi):
            return window[:].indirect(index[:, lo // STRIPE : hi // STRIPE])

        def pick(engine, dst, window, index, lo, hi):
            if engine is nc.vector:
                nc.vector.tensor_copy(out=dst, in_=looked_up(window, index, lo, hi))
            else:
                nc.scalar.activation(out=dst, in_=looked_up(window, index, lo, hi), func=COPY)

        def weave(copy, dst, src):
            copy(out=dst.rearrange("p (c i) j -> p c j i", i=RUN), in_=src.rearrange("p j (c i) -> p c j i", i=RUN))

        def quantise(values, name, offset=None):
            width = values.shape[1]
            if offset is None:
                codes = keep.tile([P, width], U32, align_bytes=64, name="codes_" + name)
            else:
                codes = reuse.tile([P, width], U32, align_bytes=64, offset=offset, name="codes_" + name)
            scales = keep.tile([P, width], U8, align_bytes=64, name="scales_" + name)
            nc.vector.quantize_mx(out=codes[:].bitcast(FP8X4), scales=scales[:], in_=values.rearrange("p s j -> p (s j)"))
            return codes, scales

        w_woven = [keep.tile([P, N, PACK], BF16, align_bytes=64, name="w_woven_%d" % g) for g in range(PASSES)]

        gate_bank = psum.tile([P, P], F32, name="sum_0")
        nc.tensor.transpose(gate_bank[:], gate_rows[:], ident[:])
        gates_turned = gate_bank[:, 0 : D * HALVES * SPREAD : SPREAD].rearrange("p (d h) -> p h d", h=HALVES)
        gates01 = keep.tile([P, HALVES, 2], F32)
        centre = keep.tile([P, HALVES], F32)
        summands = keep.tile([P, HALVES, D], F32)
        nc.scalar.copy(out=gates01[:], in_=gates_turned[:, :, 0:2])
        for h in range(HALVES):
            nc.scalar.activation(out=summands[:, h, :], in_=gates_turned[:, h, 0:D], func=COPY, scale=-1.0, bias=1.0 / D, accum_out=centre[:, h : h + 1])

        def pick_first_row(dst, g, j):
            for h in range(2):
                pick(nc.scalar, dst[:, h, j, :], loaded[g, j], offs_sb, h * HALF, (h + 1) * HALF)

        def pick_pair(dst, g, j):
            pick_first_row(dst, g, j)
            nc.vector.tensor_copy(out=dst[:, :, j + 1, :], in_=loaded[g, j][:, T : 2 * T].indirect(offs_sb[:]))

        picked0 = keep.tile([P, 2, PACK, HALF], BF16)
        woven0 = keep.tile([P, S, PACK], BF16, align_bytes=64)
        for j in (0, 2):
            pick_pair(picked0, 0, j)
        for h in range(2):
            weave(nc.vector.tensor_copy, woven0[:, h * HALF : (h + 1) * HALF, :], picked0[:, h, :, :])
        first_pass = [quantise(woven0[:, lo : lo + HALF, :], "x0_%d" % lo) for lo in (0, HALF)]

        picked1 = keep.tile([P, PACK, S], BF16)
        woven1 = woven0

        def pick_plane(engine, j, lo, hi):
            pick(engine, picked1[:, j, lo:hi], loaded[1, j], offs_sb, lo, hi)

        pick_plane(nc.scalar, 0, 0, S)
        pick_plane(nc.scalar, 1, 0, S)
        pick_plane(nc.vector, 2, 0, VECTOR_SHARE_1_2)
        pick_plane(nc.scalar, 2, VECTOR_SHARE_1_2, S)
        pick_plane(nc.vector, 3, 0, QUARTER)
        pick_plane(nc.vector, 3, QUARTER, HALF)
        pick_plane(nc.scalar, 3, HALF, S)
        for g in range(PASSES):
            weave(nc.scalar.copy, w_woven[g][:], w_raw[g][:])
        for lo, hi in ((0, QUARTER), (QUARTER, HALF), (HALF, HALF + QUARTER)):
            weave(nc.vector.tensor_copy, woven1[:, lo:hi, :], picked1[:, :, lo:hi])
        groups = ((0, HALF), (HALF, HALF + QUARTER), (HALF + QUARTER, S))
        weights = [quantise(w_woven[0][:], "w0")]
        last_pass = [quantise(woven1[:, 0:HALF, :], "x1_0", w_at + w_bytes // 2)]
        woven_last = w_woven[0]
        split = QUARTER - SCALAR_WEAVES
        weave(nc.vector.tensor_copy, woven_last[:, 0:split, :], picked1[:, :, S - QUARTER : S - QUARTER + split])
        weave(nc.scalar.copy, woven_last[:, split:QUARTER, :], picked1[:, :, S - QUARTER + split : S])
        weights.append(quantise(w_woven[1][:], "w1"))
        last_pass.append(quantise(woven1[:, HALF : HALF + QUARTER, :], "x1_2", w_at + w_bytes))
        last_pass.append(quantise(woven_last[:], "x1_3", w_at + w_bytes + w_bytes // 2))

        def product(acc, g, codes, scales):
            nc.tensor.matmul_mx(
                out=acc[:],
                lhsT=weights[g][0][:].bitcast(FP8X4),
                lhsT_scale=weights[g][1][:],
                rhs=codes.bitcast(FP8X4),
                rhs_scale=scales,
                start=(g == 0),
                stop=(g == PASSES - 1),
            )

        accs = [psum.tile([P, hi - lo], F32, name="acc_%d" % i) for i, (lo, hi) in enumerate(groups)]
        for acc, (lo, hi) in zip(accs, groups):
            codes, scales = first_pass[lo // HALF]
            within = slice(lo % HALF, (hi - 1) % HALF + 1)
            product(acc, 0, codes[:, within], scales[:, within])
        y = keep.tile([P, S], F32)
        copies_out = (nc.scalar.copy, nc.vector.tensor_copy, nc.scalar.copy)
        for acc, (lo, hi), (codes, scales), copy in zip(accs, groups, last_pass, copies_out):
            product(acc, 1, codes[:], scales[:])
            copy(out=y[:, lo:hi], in_=acc[:])

        halves = [slice(h * P, (h + 1) * P) for h in range(HALVES)]
        at_cen = keep.tile([P, V], F32)
        at_pos1 = keep.tile([P, V], F32)
        at_pos2_lower = keep.tile([P, P], F32)
        pick(nc.vector, at_pos2_lower[:], y, list_sb["pos2"], 0, P)
        pick(nc.scalar, at_cen[:], y, list_sb["cen"], 0, V)
        pick(nc.scalar, at_pos1[:, 0:P], y, list_sb["pos1"], 0, P)
        pick(nc.scalar, at_pos1[:, P:V], y, list_sb["pos1"], P, V)
        turns = [(at_pos2_lower[:], gates01[:, 0, 1:2], 0, "acc_2")]
        turns += [(at_cen[:, halves[h]], centre[:, h : h + 1], h, "turned_%d" % h) for h in range(HALVES)]
        turns += [(at_pos1[:, halves[h]], gates01[:, h, 0:1], h, "acc_%d" % h) for h in range(HALVES)]
        turned = []
        for values, factor, h, bank_name in turns:
            bank = psum.tile([P, P], F32, name=bank_name)
            nc.tensor.transpose(bank[:], values, ident[:])
            turned.append(bank)
        weighed = []
        for i, (values, factor, h, bank_name) in enumerate(turns):
            scaled = keep.tile([P, P], F32, name="weighed_%d" % i)
            nc.scalar.activation(out=scaled[:], in_=turned[i][:], func=COPY, scale=factor)
            weighed.append(scaled)
        sums = [psum.tile([P, P], F32, name="sum_%d" % h) for h in range(HALVES)]
        half_of = [turn[2] for turn in turns]
        for i, h in enumerate(half_of):
            opens, closes = h not in half_of[:i], h not in half_of[i + 1 :]
            nc.tensor.matmul(sums[h][:], weighed[i][:], ident[:], start=opens, stop=closes, is_transpose=True)

        pos2_upper = keep.tile([P, P], F32)
        nc.vector.tensor_tensor(pos2_upper[:], looked_up(y, list_sb["pos2"], P, V), gate1_upper[:], MULT)
        products = []
        for d, name in enumerate(("pos3", "pos4")):
            term = keep.tile([P, V], F32, name="term_" + name)
            nc.vector.tensor_tensor(term[:], looked_up(y, list_sb[name], 0, V), gates23[:, d, :], MULT)
            products.append(term)
        upper_part = keep.tile([P, P], F32)
        nc.vector.tensor_tensor(upper_part[:], pos2_upper[:], products[0][:, halves[1]], ADD)
        fused = [keep.tile([P, P], F32, name="fused_%d" % h) for h in range(HALVES)]
        nc.vector.tensor_tensor(fused[0][:], products[0][:, halves[0]], products[1][:, halves[0]], ADD)
        nc.vector.tensor_tensor(fused[1][:], upper_part[:], products[1][:, halves[1]], ADD)
        for h, queue in enumerate((nc.sync, nc.sync)):
            result = keep.tile([P, P], F32, name="result_%d" % h)
            nc.vector.tensor_tensor(result[:], sums[h][:], fused[h][:], ADD)
            queue.dma_start(out=out[:, halves[h]], in_=result[:])
